import numpy as np
import ml_dtypes


def mxq(x, axis, fmt="e4m3"):
    dtype, down = {"e4m3": (ml_dtypes.float8_e4m3fn, 7), "e5m2": (ml_dtypes.float8_e5m2, 14)}[fmt]
    v = np.moveaxis(np.asarray(x, np.float32).astype(ml_dtypes.bfloat16).astype(np.float64), axis, -1)
    blocks = v.reshape(v.shape[:-1] + (-1, 32))
    amax = np.abs(blocks).max(-1, keepdims=True)
    byte = np.maximum(np.where(amax > 0, np.frexp(amax)[1] - 1 + 127, 0) - down, 1)
    scale = np.exp2(byte - 127.0)
    codes = (blocks / scale).astype(np.float32).astype(dtype).astype(np.float64)
    return np.moveaxis((codes * scale).reshape(v.shape), -1, axis)


WIDE = False


def mx_kscale(k):
    if not WIDE:
        return np.ones(k)
    levels = np.array([10, -10, 5, -5, 0])
    if k % 512:
        return np.exp2(np.random.permutation(np.resize(levels, k // 32))).repeat(32)
    a = np.empty((k // 512, 16))
    for p in range(k // 512):
        a[p, :8] = np.random.permutation(np.resize(levels, 8))
        for g in range(8):
            far = levels[np.abs(levels - a[p, g]) >= 10]
            a[p, g + 8] = far[np.random.randint(len(far))]
    return np.exp2(a.ravel()).repeat(32)


BF16 = ml_dtypes.bfloat16


def bf(x):
    return np.asarray(x, np.float32).astype(BF16)


def f64(x):
    return np.asarray(x).astype(np.float64)


N, D, L, K, O = 4096, 512, 512, 3, 256


def smooth_reciprocal(z):
    return z / (z * z + 0.5)


def draw0():
    s, t = mx_kscale(D), mx_kscale(L)
    return {
        "x": bf(np.random.standard_normal((N, D)) * s),
        "w0": bf(np.random.standard_normal((D, L)) / np.sqrt(D) / s[:, None]),
        "w1": bf(np.random.standard_normal((D, L)) / np.sqrt(D) / s[:, None]),
        "w2": bf(np.random.standard_normal((D, L)) / np.sqrt(D) / s[:, None]),
        "b": bf(0.3 * np.random.standard_normal((K, L))),
        "g": bf((1.0 + 0.1 * np.random.standard_normal(L)) * t),
        "v": bf(np.random.standard_normal((L, O)) / np.sqrt(L) / t[:, None]),
    }


def core(x, w0, w1, w2, b, g, v):
    b = f64(b)
    xq = mxq(f64(x), 1, "e4m3")
    a0 = (xq @ mxq(f64(w0), 0, "e4m3")) + b[0]
    a1 = (xq @ mxq(f64(w1), 0, "e4m3")) + b[1]
    a2 = (xq @ mxq(f64(w2), 0, "e4m3")) + b[2]
    f1 = a1 + smooth_reciprocal(a2)
    f0 = a0 + smooth_reciprocal(f1)
    h = f0 * f64(g)[None, :]
    return mxq(h, 1, "e4m3") @ mxq(f64(v), 0, "e4m3")


def e4m3fn_bytes(y):
    return np.clip(np.asarray(y, np.float64), -448.0, 448.0).astype(np.float32).astype(ml_dtypes.float8_e4m3fn).view(np.uint8)


def e4m3fn_values(b):
    return np.asarray(b, np.uint8).view(ml_dtypes.float8_e4m3fn).astype(np.float64)


def setup_inputs():
    d = draw0()
    x0 = np.asarray(d['x']).astype(np.float64)
    s = (np.max(np.abs(x0), axis=(0,), keepdims=True) / 448.0).astype(np.float32)
    out = {}
    for k, v in d.items():
        if k == 'x':
            out['x_bytes'] = e4m3fn_bytes(x0 / s.astype(np.float64))
            out['x_scale'] = s
        else:
            out[k] = v
    return out


def reference(x_bytes, x_scale, w0, w1, w2, b, g, v):
    return core(e4m3fn_values(x_bytes) * x_scale.astype(np.float64), w0, w1, w2, b, g, v)

@@ -1,0 +1,339 @@
+from contextlib import ExitStack
+
+import concourse.mybir as mybir
+from concourse.masks import make_identity
+
+N, D, L, O = 4096, 512, 512, 256
+FLOPS = 2 * N * D * L * 3 + 2 * N * L * O
+
+F32 = mybir.dt.float32
+BF16 = mybir.dt.bfloat16
+U32 = mybir.dt.uint32
+U8 = mybir.dt.uint8
+FP8 = mybir.dt.float8_e4m3fn
+FP8X4 = mybir.dt.float8_e4m3fn_x4
+ADD = mybir.AluOpType.add
+MULT = mybir.AluOpType.mult
+ACT = mybir.ActivationFunctionType
+
+P = 128
+T = 4
+BLK = 512
+NB = N // BLK
+UNITS = NB * T
+
+
+def tile_cofrnetladderlayer_t_kernel(tc, x_bytes, x_scale, w0, w1, w2, b, g, v, out):
+    nc = tc.nc
+    with ExitStack() as ctx:
+        keep = ctx.enter_context(tc.tile_pool(name="keep", bufs=1))
+        xin = ctx.enter_context(tc.tile_pool(name="xin", bufs=NB))
+        two = ctx.enter_context(tc.tile_pool(name="two", bufs=2))
+        three = ctx.enter_context(tc.tile_pool(name="three", bufs=3))
+        four = ctx.enter_context(tc.tile_pool(name="four", bufs=4))
+        p_a2 = ctx.enter_context(tc.psum_pool(name="p_a2", bufs=3))
+        p_a1 = ctx.enter_context(tc.psum_pool(name="p_a1", bufs=1))
+        p_a0 = ctx.enter_context(tc.psum_pool(name="p_a0", bufs=1))
+        p_xt = ctx.enter_context(tc.psum_pool(name="p_xt", bufs=2))
+        p_out = ctx.enter_context(tc.psum_pool(name="p_out", bufs=1))
+        ctx.enter_context(tc.manual_schedule())
+
+        scale_x = keep.tile([P, T], F32, name="scale_x")
+        nc.scalar.dma_start(out=scale_x[:], in_=x_scale.rearrange("o (p t) -> p (o t)", t=T))
+        b_raw = keep.tile([P, 3, T], BF16, name="b_raw")
+        nc.scalar.dma_start(out=b_raw[:], in_=b.rearrange("i (p t) -> p i t", t=T))
+        g_raw = keep.tile([P, T], BF16, name="g_raw")
+        nc.scalar.dma_start(out=g_raw[:], in_=g.rearrange("(p t) -> p t", t=T))
+
+        x8 = {}
+
+        def load_x(blk):
+            x8[blk] = xin.tile([P, T, D], U8, name="x8")
+            rows = x_bytes[blk * BLK : (blk + 1) * BLK, :]
+            nc.sync.dma_start(out=x8[blk][:], in_=rows.rearrange("(p r) k -> p r k", r=T))
+
+        def load_w(w, name):
+            raw = keep.tile([P, T, w.shape[1]], BF16, name="raw_" + name)
+            nc.sync.dma_start(out=raw[:], in_=w.rearrange("(p j) c -> p j c", j=T))
+            return raw
+
+        load_x(0)
+        raw2 = load_w(w2, "w2")
+        raw1 = load_w(w1, "w1")
+        load_x(1)
+        raw0 = load_w(w0, "w0")
+        raw_v = load_w(v, "v")
+        for blk in range(2, NB):
+            load_x(blk)
+
+        ident = keep.tile([P, P], F32, name="ident")
+        make_identity(nc, ident[:])
+
+        warm = keep.tile([P, 1], F32, name="warm")
+        nc.vector.memset(warm[:], 1.0)
+        warm_out = keep.tile([P, 1], F32, name="warm_out")
+        nc.scalar.activation(out=warm_out[:], in_=warm[:], func=ACT.Abs_reciprocal_sqrt)
+
+        bias = keep.tile([P, 3, T], F32, name="bias")
+        nc.vector.tensor_copy(out=bias[:], in_=b_raw[:])
+        gain = keep.tile([P, T], F32, name="gain")
+        nc.vector.tensor_copy(out=gain[:], in_=g_raw[:])
+
+        xb, xt, xs, xq, xqs = {}, {}, {}, {}, {}
+
+        def cast_x(blk):
+            xb[blk] = two.tile([P, T, D], BF16, name="xb")
+            nc.vector.tensor_copy(out=xb[blk][:], in_=x8[blk][:].bitcast(FP8))
+
+        def transpose_x(blk, half):
+            words = xb[blk][:].bitcast(F32)
+            bank = p_xt.tile([P, 2, 2 * P], F32, name="xt")
+            xt[blk, half] = bank
+            for i in range(2):
+                for u in range(2):
+                    nc.tensor.transpose(
+                        bank[:, u, i * P : (i + 1) * P], words[:, 2 * half + i, u : D // 2 : 2], ident[:]
+                    )
+
+        def scale_x_half(blk, half):
+            if half == 0:
+                xs[blk] = two.tile([P, BLK, T], BF16, name="xs", align_bytes=64)
+            cols = xs[blk][:, half * 2 * P : (half + 1) * 2 * P, :]
+            nc.vector.tensor_tensor(
+                out=cols.rearrange("p m (u e) -> p m u e", e=2),
+                in0=xt[blk, half][:].bitcast(BF16).rearrange("p u (m e) -> p m u e", e=2),
+                in1=scale_x[:].unsqueeze(1).to_broadcast([P, 2 * P, T]).rearrange("p m (u e) -> p m u e", e=2),
+                op=MULT,
+            )
+
+        def quantize_x(blk):
+            xq[blk] = three.tile([P, BLK], U32, name="xq", align_bytes=64)
+            xqs[blk] = three.tile([P, BLK], U8, name="xqs", align_bytes=64)
+            nc.vector.quantize_mx(
+                out=xq[blk][:].bitcast(FP8X4),
+                scales=xqs[blk][:],
+                in_=xs[blk][:].rearrange("p m t -> p (m t)"),
+            )
+
+        def weight_tiles(name, width):
+            return (
+                keep.tile([P, T * width], BF16, name="grp_" + name, align_bytes=64),
+                keep.tile([P, width], U32, name="cod_" + name, align_bytes=64),
+                keep.tile([P, width], U8, name="sca_" + name, align_bytes=64),
+            )
+
+        def quantize_w(tiles, c0, c1):
+            grp, cod, sca = tiles
+            nc.vector.quantize_mx(
+                out=cod[:, c0:c1].bitcast(FP8X4), scales=sca[:, c0:c1], in_=grp[:, T * c0 : T * c1]
+            )
+
+        tw2 = weight_tiles("w2", L)
+        tw1 = weight_tiles("w1", L)
+        tw0 = weight_tiles("w0", L)
+        tv = weight_tiles("v", O)
+
+        def permuted(raw):
+            return raw[:].rearrange("p j (m t) -> p t m j", t=T)
+
+        def grouped(tiles):
+            return tiles[0][:].rearrange("p (t m j) -> p t m j", t=T, j=T)
+
+        a2, a1, a0 = {}, {}, {}
+        w2t, r2, f1, w1t, r1, f0 = {}, {}, {}, {}, {}, {}
+
+        def rung_matmul(pool, name, tiles, u):
+            blk, t = divmod(u, T)
+            bank = pool.tile([P, BLK], F32, name=name)
+            cols = slice(t * P, (t + 1) * P)
+            nc.tensor.matmul_mx(
+                out=bank[:],
+                lhsT=tiles[1][:, cols].bitcast(FP8X4),
+                lhsT_scale=tiles[2][:, cols],
+                rhs=xq[blk][:].bitcast(FP8X4),
+                rhs_scale=xqs[blk][:],
+                start=True,
+                stop=True,
+            )
+            return bank
+
+        def b_col(i, u):
+            t = u % T
+            return bias[:, i, t : t + 1]
+
+        def act(out_pool, name, src, func, bias_in):
+            dst = out_pool.tile([P, BLK], F32, name=name)
+            nc.scalar.activation(out=dst[:], in_=src[:], func=func, bias=bias_in)
+            return dst
+
+        hh, hq, hqs, po, osb = {}, {}, {}, {}, {}
+
+        def gain_piece(eng, blk, q, width):
+            if q == 0:
+                hh[blk] = two.tile([P, BLK, T], BF16, name="hh", align_bytes=64)
+            n = slice(q * width, (q + 1) * width)
+            eng.tensor_tensor(
+                out=hh[blk][:, n, :].rearrange("p (c i) t -> p c t i", i=4),
+                in0=f0[blk][:, :, n].rearrange("p t (c i) -> p c t i", i=4),
+                in1=gain[:].unsqueeze(1).unsqueeze(3).to_broadcast([P, width // 4, T, 4]),
+                op=MULT,
+            )
+
+        def quantize_h(blk, half):
+            if half == 0:
+                hq[blk] = two.tile([P, BLK], U32, name="hq", align_bytes=64)
+                hqs[blk] = two.tile([P, BLK], U8, name="hqs", align_bytes=64)
+            n = slice(half * 256, (half + 1) * 256)
+            nc.vector.quantize_mx(
+                out=hq[blk][:, n].bitcast(FP8X4),
+                scales=hqs[blk][:, n],
+                in_=hh[blk][:, n, :].rearrange("p m t -> p (m t)"),
+            )
+
+        def mix(blk, half):
+            po[blk, half] = p_out.tile([P, 2, O], F32, name="po")
+            for i in range(2):
+                r = 2 * half + i
+                rows = slice(r * P, (r + 1) * P)
+                nc.tensor.matmul_mx(
+                    out=po[blk, half][:, i, :],
+                    lhsT=hq[blk][:, rows].bitcast(FP8X4),
+                    lhsT_scale=hqs[blk][:, rows],
+                    rhs=tv[1][:].bitcast(FP8X4),
+                    rhs_scale=tv[2][:],
+                    start=True,
+                    stop=True,
+                )
+
+        def store(blk, half, evict):
+            if half == 0:
+                osb[blk] = three.tile([P, T, O], F32, name="osb")
+            rs = slice(2 * half, 2 * half + 2)
+            evict(out=osb[blk][:, rs, :], in_=po[blk, half][:])
+            dst = out[blk * BLK : (blk + 1) * BLK, :].rearrange("(p r) o -> p r o", r=T)
+            nc.sync.dma_start(out=dst[:, rs, :], in_=osb[blk][:, rs, :])
+
+        cast_x(0)
+        transpose_x(0, 0)
+        transpose_x(0, 1)
+        nc.scalar.copy(out=grouped(tw1), in_=permuted(raw1))
+        nc.gpsimd.tensor_scalar(out=grouped(tw0), in0=permuted(raw0), scalar1=1.0, scalar2=0.0, op0=MULT, op1=ADD)
+        nc.gpsimd.tensor_scalar(
+            out=tv[0][:].rearrange("p (c j) -> p c j", j=T),
+            in0=raw_v[:].rearrange("p j c -> p c j"),
+            scalar1=1.0,
+            scalar2=0.0,
+            op0=MULT,
+            op1=ADD,
+        )
+
+        def copy_w2(t):
+            nc.vector.tensor_copy(out=grouped(tw2)[:, t], in_=permuted(raw2)[:, t])
+
+        scale_x_half(0, 0)
+        copy_w2(0)
+        scale_x_half(0, 1)
+        quantize_w(tw2, 0, P)
+        quantize_x(0)
+        a2[0] = rung_matmul(p_a2, "a2", tw2, 0)
+        copy_w2(1)
+        copy_w2(2)
+        quantize_w(tw2, P, 2 * P)
+        copy_w2(3)
+        cast_x(1)
+        quantize_w(tw2, 2 * P, L)
+        quantize_w(tw1, 0, L)
+
+        for i in range(UNITS + 2):
+            k = i % T
+            if i + 1 < UNITS:
+                a2[i + 1] = rung_matmul(p_a2, "a2", tw2, i + 1)
+            if 0 <= i - 1 < UNITS:
+                a1[i - 1] = rung_matmul(p_a1, "a1", tw1, i - 1)
+            if 0 <= i - 3 < UNITS:
+                a0[i - 3] = rung_matmul(p_a0, "a0", tw0, i - 3)
+            nxt = i // T + 1
+            if k == 0 and nxt < NB:
+                transpose_x(nxt, 0)
+                transpose_x(nxt, 1)
+
+            if i < UNITS:
+                q2 = act(three, "q2", a2[i], ACT.Square, b_col(2, i))
+            if 0 <= i - 2 < UNITS:
+                q1 = act(three, "q1", f1[i - 2], ACT.Square, 0.0)
+            if i < UNITS:
+                s2 = act(three, "s2", q2, ACT.Abs_reciprocal_sqrt, 0.5)
+            if 0 <= i - 2 < UNITS:
+                s1 = act(three, "s1", q1, ACT.Abs_reciprocal_sqrt, 0.5)
+            if i < UNITS:
+                w2t[i] = act(three, "w2t", s2, ACT.Square, 0.0)
+            if 0 <= i - 2 < UNITS:
+                w1t[i - 2] = act(three, "w1t", s1, ACT.Square, 0.0)
+
+            if 0 <= i - 3 < UNITS:
+                u = i - 3
+                r1[u] = two.tile([P, BLK], F32, name="r1")
+                nc.gpsimd.tensor_tensor(out=r1[u][:], in0=f1[u][:], in1=w1t[u][:], op=MULT)
+            hb, hp = divmod(i - 7, T)
+            if 0 <= hb < NB - 1:
+                gain_piece(nc.gpsimd, hb, hp, P)
+
+            if 0 <= i - 1 < UNITS:
+                u = i - 1
+                r2[u] = two.tile([P, BLK], F32, name="r2")
+                nc.vector.scalar_tensor_tensor(
+                    out=r2[u][:], in0=a2[u][:], scalar=b_col(2, u), in1=w2t[u][:], op0=ADD, op1=MULT
+                )
+            if k < 2 and nxt < NB:
+                scale_x_half(nxt, k)
+            if k == 2 and nxt < NB:
+                quantize_x(nxt)
+            if i == 0:
+                quantize_w(tw0, 0, L)
+            if i == 1:
+                quantize_w(tv, 0, O)
+            if 0 <= i - 1 < UNITS:
+                u = i - 1
+                f1[u] = four.tile([P, BLK], F32, name="f1")
+                nc.vector.scalar_tensor_tensor(
+                    out=f1[u][:], in0=a1[u][:], scalar=b_col(1, u), in1=r2[u][:], op0=ADD, op1=ADD
+                )
+            if k == 3 and nxt + 1 < NB:
+                cast_x(nxt + 1)
+            ob, op = divmod(i - 9, T)
+            if 0 <= ob < NB - 1 and op in (0, 2):
+                quantize_h(ob, op // 2)
+                mix(ob, op // 2)
+            sb, sp = divmod(i - 10, T)
+            if 0 <= sb < NB - 1 and sp in (0, 2):
+                store(sb, sp // 2, nc.vector.tensor_copy)
+            if 0 <= i - 3 < UNITS:
+                u = i - 3
+                blk, t = divmod(u, T)
+                if t == 0:
+                    f0[blk] = three.tile([P, T, BLK], F32, name="f0")
+                nc.vector.scalar_tensor_tensor(
+                    out=f0[blk][:, t, :], in0=a0[u][:], scalar=b_col(0, u), in1=r1[u][:], op0=ADD, op1=ADD
+                )
+
+        last, u = NB - 1, UNITS - 1
+        a0[u] = rung_matmul(p_a0, "a0", tw0, u)
+        gain_piece(nc.gpsimd, last - 1, T - 1, P)
+        store(last - 1, 0, nc.scalar.copy)
+        r1[u] = two.tile([P, BLK], F32, name="r1")
+        halves = (slice(0, 256), slice(256, 512))
+        for n in halves:
+            nc.vector.tensor_tensor(out=r1[u][:, n], in0=f1[u][:, n], in1=w1t[u][:, n], op=MULT)
+        for n in halves:
+            nc.vector.scalar_tensor_tensor(
+                out=f0[last][:, T - 1, n], in0=a0[u][:, n], scalar=b_col(0, u), in1=r1[u][:, n], op0=ADD, op1=ADD
+            )
+        quantize_h(last - 1, 1)
+        mix(last - 1, 1)
+        store(last - 1, 1, nc.scalar.copy)
+        gain_piece(nc.vector, last, 0, 256)
+        gain_piece(nc.vector, last, 1, 256)
+        for half in range(2):
+            quantize_h(last, half)
+            mix(last, half)
+            store(last, half, nc.scalar.copy)

@@ -18,8 +18,9 @@ ACT = mybir.ActivationFunctionType
 
 P = 128
 T = 4
-BLK = 512
-NB = N // BLK
+WIDTHS = (256, 512, 512, 512, 512, 512, 512, 512, 256)
+NB = len(WIDTHS)
+STARTS = tuple(sum(WIDTHS[:i]) for i in range(NB))
 UNITS = NB * T
 
 
@@ -28,9 +29,9 @@ def tile_cofrnetladderlayer_t_kernel(tc, x_bytes, x_scale, w0, w1, w2, b, g, v, 
     with ExitStack() as ctx:
         keep = ctx.enter_context(tc.tile_pool(name="keep", bufs=1))
         xin = ctx.enter_context(tc.tile_pool(name="xin", bufs=NB))
-        two = ctx.enter_context(tc.tile_pool(name="two", bufs=2))
-        three = ctx.enter_context(tc.tile_pool(name="three", bufs=3))
-        four = ctx.enter_context(tc.tile_pool(name="four", bufs=4))
+        two = ctx.enter_context(tc.tile_pool(name="two", bufs=3))
+        three = ctx.enter_context(tc.tile_pool(name="three", bufs=4))
+        four = ctx.enter_context(tc.tile_pool(name="four", bufs=5))
         p_a2 = ctx.enter_context(tc.psum_pool(name="p_a2", bufs=3))
         p_a1 = ctx.enter_context(tc.psum_pool(name="p_a1", bufs=1))
         p_a0 = ctx.enter_context(tc.psum_pool(name="p_a0", bufs=1))
@@ -38,19 +39,13 @@ def tile_cofrnetladderlayer_t_kernel(tc, x_bytes, x_scale, w0, w1, w2, b, g, v, 
         p_out = ctx.enter_context(tc.psum_pool(name="p_out", bufs=1))
         ctx.enter_context(tc.manual_schedule())
 
-        scale_x = keep.tile([P, T], F32, name="scale_x")
-        nc.scalar.dma_start(out=scale_x[:], in_=x_scale.rearrange("o (p t) -> p (o t)", t=T))
-        b_raw = keep.tile([P, 3, T], BF16, name="b_raw")
-        nc.scalar.dma_start(out=b_raw[:], in_=b.rearrange("i (p t) -> p i t", t=T))
-        g_raw = keep.tile([P, T], BF16, name="g_raw")
-        nc.scalar.dma_start(out=g_raw[:], in_=g.rearrange("(p t) -> p t", t=T))
-
         x8 = {}
 
         def load_x(blk):
-            x8[blk] = xin.tile([P, T, D], U8, name="x8")
-            rows = x_bytes[blk * BLK : (blk + 1) * BLK, :]
-            nc.sync.dma_start(out=x8[blk][:], in_=rows.rearrange("(p r) k -> p r k", r=T))
+            width = WIDTHS[blk]
+            x8[blk] = xin.tile([P, width // P, D], U8, name="x8")
+            rows = x_bytes[STARTS[blk] : STARTS[blk] + width, :]
+            nc.sync.dma_start(out=x8[blk][:], in_=rows.rearrange("(p r) k -> p r k", p=P))
 
         def load_w(w, name):
             raw = keep.tile([P, T, w.shape[1]], BF16, name="raw_" + name)
@@ -62,9 +57,17 @@ def tile_cofrnetladderlayer_t_kernel(tc, x_bytes, x_scale, w0, w1, w2, b, g, v, 
         raw1 = load_w(w1, "w1")
         load_x(1)
         raw0 = load_w(w0, "w0")
+        load_x(2)
         raw_v = load_w(v, "v")
-        for blk in range(2, NB):
+        for blk in range(3, NB):
             load_x(blk)
+
+        scale_x = keep.tile([P, T], F32, name="scale_x")
+        nc.scalar.dma_start(out=scale_x[:], in_=x_scale.rearrange("o (p t) -> p (o t)", t=T))
+        b_raw = keep.tile([P, 3, T], BF16, name="b_raw")
+        nc.scalar.dma_start(out=b_raw[:], in_=b.rearrange("i (p t) -> p i t", t=T))
+        g_raw = keep.tile([P, T], BF16, name="g_raw")
+        nc.scalar.dma_start(out=g_raw[:], in_=g.rearrange("(p t) -> p t", t=T))
 
         ident = keep.tile([P, P], F32, name="ident")
         make_identity(nc, ident[:])
@@ -74,45 +77,38 @@ def tile_cofrnetladderlayer_t_kernel(tc, x_bytes, x_scale, w0, w1, w2, b, g, v, 
         warm_out = keep.tile([P, 1], F32, name="warm_out")
         nc.scalar.activation(out=warm_out[:], in_=warm[:], func=ACT.Abs_reciprocal_sqrt)
 
-        bias = keep.tile([P, 3, T], F32, name="bias")
-        nc.vector.tensor_copy(out=bias[:], in_=b_raw[:])
-        gain = keep.tile([P, T], F32, name="gain")
-        nc.vector.tensor_copy(out=gain[:], in_=g_raw[:])
-
         xb, xt, xs, xq, xqs = {}, {}, {}, {}, {}
 
-        def cast_x(blk):
-            xb[blk] = two.tile([P, T, D], BF16, name="xb")
-            nc.vector.tensor_copy(out=xb[blk][:], in_=x8[blk][:].bitcast(FP8))
+        def cast_x(copy, blk, r):
+            if r == 0:
+                xb[blk] = two.tile([P, WIDTHS[blk] // P, D], BF16, name="xb")
+            copy(out=xb[blk][:, r, :], in_=x8[blk][:, r, :].bitcast(FP8))
 
-        def transpose_x(blk, half):
+        def transpose_x(blk, r):
             words = xb[blk][:].bitcast(F32)
-            bank = p_xt.tile([P, 2, 2 * P], F32, name="xt")
-            xt[blk, half] = bank
-            for i in range(2):
-                for u in range(2):
-                    nc.tensor.transpose(
-                        bank[:, u, i * P : (i + 1) * P], words[:, 2 * half + i, u : D // 2 : 2], ident[:]
-                    )
+            xt[blk, r] = p_xt.tile([P, 2, P], F32, name="xt")
+            for u in range(2):
+                nc.tensor.transpose(xt[blk, r][:, u, :], words[:, r, u : D // 2 : 2], ident[:])
 
-        def scale_x_half(blk, half):
-            if half == 0:
-                xs[blk] = two.tile([P, BLK, T], BF16, name="xs", align_bytes=64)
-            cols = xs[blk][:, half * 2 * P : (half + 1) * 2 * P, :]
+        def scale_x_tile(blk, r):
+            if r == 0:
+                xs[blk] = two.tile([P, WIDTHS[blk], T], BF16, name="xs", align_bytes=64)
             nc.vector.tensor_tensor(
-                out=cols.rearrange("p m (u e) -> p m u e", e=2),
-                in0=xt[blk, half][:].bitcast(BF16).rearrange("p u (m e) -> p m u e", e=2),
-                in1=scale_x[:].unsqueeze(1).to_broadcast([P, 2 * P, T]).rearrange("p m (u e) -> p m u e", e=2),
+                out=xs[blk][:, r * P : (r + 1) * P, :].rearrange("p m (u e) -> p m u e", e=2),
+                in0=xt[blk, r][:].bitcast(BF16).rearrange("p u (m e) -> p m u e", e=2),
+                in1=scale_x[:].unsqueeze(1).to_broadcast([P, P, T]).rearrange("p m (u e) -> p m u e", e=2),
                 op=MULT,
             )
 
-        def quantize_x(blk):
-            xq[blk] = three.tile([P, BLK], U32, name="xq", align_bytes=64)
-            xqs[blk] = three.tile([P, BLK], U8, name="xqs", align_bytes=64)
+        def quantize_x(blk, r0, r1):
+            if r0 == 0:
+                xq[blk] = three.tile([P, WIDTHS[blk]], U32, name="xq", align_bytes=64)
+                xqs[blk] = three.tile([P, WIDTHS[blk]], U8, name="xqs", align_bytes=64)
+            n = slice(r0 * P, r1 * P)
             nc.vector.quantize_mx(
-                out=xq[blk][:].bitcast(FP8X4),
-                scales=xqs[blk][:],
-                in_=xs[blk][:].rearrange("p m t -> p (m t)"),
+                out=xq[blk][:, n].bitcast(FP8X4),
+                scales=xqs[blk][:, n],
+                in_=xs[blk][:, n, :].rearrange("p m t -> p (m t)"),
             )
 
         def weight_tiles(name, width):
@@ -139,12 +135,18 @@ def tile_cofrnetladderlayer_t_kernel(tc, x_bytes, x_scale, w0, w1, w2, b, g, v, 
         def grouped(tiles):
             return tiles[0][:].rearrange("p (t m j) -> p t m j", t=T, j=T)
 
+        def copy_w2(t):
+            nc.vector.tensor_copy(out=grouped(tw2)[:, t], in_=permuted(raw2)[:, t])
+
+        def copy_w0(t):
+            nc.scalar.copy(out=grouped(tw0)[:, t], in_=permuted(raw0)[:, t])
+
         a2, a1, a0 = {}, {}, {}
         w2t, r2, f1, w1t, r1, f0 = {}, {}, {}, {}, {}, {}
 
         def rung_matmul(pool, name, tiles, u):
             blk, t = divmod(u, T)
-            bank = pool.tile([P, BLK], F32, name=name)
+            bank = pool.tile([P, WIDTHS[blk]], F32, name=name)
             cols = slice(t * P, (t + 1) * P)
             nc.tensor.matmul_mx(
                 out=bank[:],
@@ -161,179 +163,210 @@ def tile_cofrnetladderlayer_t_kernel(tc, x_bytes, x_scale, w0, w1, w2, b, g, v, 
             t = u % T
             return bias[:, i, t : t + 1]
 
-        def act(out_pool, name, src, func, bias_in):
-            dst = out_pool.tile([P, BLK], F32, name=name)
+        def act(name, src, func, bias_in):
+            dst = three.tile([P, src.shape[1]], F32, name=name)
             nc.scalar.activation(out=dst[:], in_=src[:], func=func, bias=bias_in)
+            return dst
+
+        def product(eng, pool, name, a, c):
+            dst = pool.tile([P, a.shape[1]], F32, name=name)
+            eng.tensor_tensor(out=dst[:], in0=a[:], in1=c[:], op=MULT)
             return dst
 
         hh, hq, hqs, po, osb = {}, {}, {}, {}, {}
 
-        def gain_piece(eng, blk, q, width):
-            if q == 0:
-                hh[blk] = two.tile([P, BLK, T], BF16, name="hh", align_bytes=64)
-            n = slice(q * width, (q + 1) * width)
+        def gain_tile(eng, blk, r):
+            if r == 0:
+                hh[blk] = two.tile([P, WIDTHS[blk], T], BF16, name="hh", align_bytes=64)
+            n = slice(r * P, (r + 1) * P)
             eng.tensor_tensor(
                 out=hh[blk][:, n, :].rearrange("p (c i) t -> p c t i", i=4),
                 in0=f0[blk][:, :, n].rearrange("p t (c i) -> p c t i", i=4),
-                in1=gain[:].unsqueeze(1).unsqueeze(3).to_broadcast([P, width // 4, T, 4]),
+                in1=gain[:].unsqueeze(1).unsqueeze(3).to_broadcast([P, P // 4, T, 4]),
                 op=MULT,
             )
 
-        def quantize_h(blk, half):
-            if half == 0:
-                hq[blk] = two.tile([P, BLK], U32, name="hq", align_bytes=64)
-                hqs[blk] = two.tile([P, BLK], U8, name="hqs", align_bytes=64)
-            n = slice(half * 256, (half + 1) * 256)
+        def quantize_h(blk, r0, r1):
+            if r0 == 0:
+                hq[blk] = two.tile([P, WIDTHS[blk]], U32, name="hq", align_bytes=64)
+                hqs[blk] = two.tile([P, WIDTHS[blk]], U8, name="hqs", align_bytes=64)
+            n = slice(r0 * P, r1 * P)
             nc.vector.quantize_mx(
                 out=hq[blk][:, n].bitcast(FP8X4),
                 scales=hqs[blk][:, n],
                 in_=hh[blk][:, n, :].rearrange("p m t -> p (m t)"),
             )
 
-        def mix(blk, half):
-            po[blk, half] = p_out.tile([P, 2, O], F32, name="po")
-            for i in range(2):
-                r = 2 * half + i
-                rows = slice(r * P, (r + 1) * P)
-                nc.tensor.matmul_mx(
-                    out=po[blk, half][:, i, :],
-                    lhsT=hq[blk][:, rows].bitcast(FP8X4),
-                    lhsT_scale=hqs[blk][:, rows],
-                    rhs=tv[1][:].bitcast(FP8X4),
-                    rhs_scale=tv[2][:],
-                    start=True,
-                    stop=True,
-                )
+        def mix(blk, r):
+            po[blk, r] = p_out.tile([P, O], F32, name="po")
+            rows = slice(r * P, (r + 1) * P)
+            nc.tensor.matmul_mx(
+                out=po[blk, r][:],
+                lhsT=hq[blk][:, rows].bitcast(FP8X4),
+                lhsT_scale=hqs[blk][:, rows],
+                rhs=tv[1][:].bitcast(FP8X4),
+                rhs_scale=tv[2][:],
+                start=True,
+                stop=True,
+            )
 
-        def store(blk, half, evict):
-            if half == 0:
-                osb[blk] = three.tile([P, T, O], F32, name="osb")
-            rs = slice(2 * half, 2 * half + 2)
-            evict(out=osb[blk][:, rs, :], in_=po[blk, half][:])
-            dst = out[blk * BLK : (blk + 1) * BLK, :].rearrange("(p r) o -> p r o", r=T)
-            nc.sync.dma_start(out=dst[:, rs, :], in_=osb[blk][:, rs, :])
+        def evict(copy, blk, r):
+            tiles = WIDTHS[blk] // P
+            if r == 0:
+                osb[blk] = three.tile([P, tiles, O], F32, name="osb")
+            copy(out=osb[blk][:, r, :], in_=po[blk, r][:])
+            if r == tiles - 1:
+                dst = out[STARTS[blk] : STARTS[blk] + WIDTHS[blk], :].rearrange("(p r) o -> p r o", p=P)
+                nc.sync.dma_start(out=dst, in_=osb[blk][:])
 
-        cast_x(0)
+        def tile_at(step):
+            blk, k = divmod(step, T)
+            if not 0 <= blk < NB:
+                return None
+            every = T * P // WIDTHS[blk]
+            return (blk, k // every) if k % every == 0 else None
+
+        cast_x(nc.vector.tensor_copy, 0, 0)
+        cast_x(nc.scalar.copy, 0, 1)
         transpose_x(0, 0)
         transpose_x(0, 1)
         nc.scalar.copy(out=grouped(tw1), in_=permuted(raw1))
-        nc.gpsimd.tensor_scalar(out=grouped(tw0), in0=permuted(raw0), scalar1=1.0, scalar2=0.0, op0=MULT, op1=ADD)
-        nc.gpsimd.tensor_scalar(
-            out=tv[0][:].rearrange("p (c j) -> p c j", j=T),
-            in0=raw_v[:].rearrange("p j c -> p c j"),
-            scalar1=1.0,
-            scalar2=0.0,
-            op0=MULT,
-            op1=ADD,
-        )
-
-        def copy_w2(t):
-            nc.vector.tensor_copy(out=grouped(tw2)[:, t], in_=permuted(raw2)[:, t])
-
-        scale_x_half(0, 0)
         copy_w2(0)
-        scale_x_half(0, 1)
+        scale_x_tile(0, 0)
         quantize_w(tw2, 0, P)
-        quantize_x(0)
+        scale_x_tile(0, 1)
+        bias = keep.tile([P, 3, T], F32, name="bias")
+        nc.vector.tensor_copy(out=bias[:], in_=b_raw[:])
+        gain = keep.tile([P, T], F32, name="gain")
+        nc.vector.tensor_copy(out=gain[:], in_=g_raw[:])
+        quantize_x(0, 0, 2)
         a2[0] = rung_matmul(p_a2, "a2", tw2, 0)
-        copy_w2(1)
-        copy_w2(2)
-        quantize_w(tw2, P, 2 * P)
-        copy_w2(3)
-        cast_x(1)
-        quantize_w(tw2, 2 * P, L)
-        quantize_w(tw1, 0, L)
 
-        for i in range(UNITS + 2):
-            k = i % T
-            if i + 1 < UNITS:
-                a2[i + 1] = rung_matmul(p_a2, "a2", tw2, i + 1)
-            if 0 <= i - 1 < UNITS:
+        def f0_matmul(u):
+            a0[u] = rung_matmul(p_a0, "a0", tw0, u)
+
+        def add_f0(u):
+            blk, t = divmod(u, T)
+            if t == 0:
+                f0[blk] = two.tile([P, T, WIDTHS[blk]], F32, name="f0")
+            nc.vector.scalar_tensor_tensor(
+                out=f0[blk][:, t, :], in0=a0[u][:], scalar=b_col(0, u), in1=r1[u][:], op0=ADD, op1=ADD
+            )
+
+        for i in range(-3, UNITS + 2):
+            new = 0 <= i < UNITS
+            mid = 0 <= i - 1 < UNITS
+            low = 0 <= i - 2 < UNITS
+            end = 0 <= i - 3 < UNITS
+            out_ = 0 <= i - 4 < UNITS
+            late = i >= UNITS - 6
+            to_cast = tile_at(i + 7)
+            to_turn = tile_at(i + 6)
+            to_scale = tile_at(i + 5)
+            to_gain = tile_at(i - 8)
+            to_code = tile_at(i - 9)
+            to_mix = tile_at(i - 10)
+
+            if mid:
                 a1[i - 1] = rung_matmul(p_a1, "a1", tw1, i - 1)
-            if 0 <= i - 3 < UNITS:
-                a0[i - 3] = rung_matmul(p_a0, "a0", tw0, i - 3)
-            nxt = i // T + 1
-            if k == 0 and nxt < NB:
-                transpose_x(nxt, 0)
-                transpose_x(nxt, 1)
+            if out_:
+                f0_matmul(i - 4)
+            if to_mix:
+                mix(*to_mix)
+            if 0 <= i and i + 1 < UNITS:
+                a2[i + 1] = rung_matmul(p_a2, "a2", tw2, i + 1)
+            if to_turn and to_turn[0] > 0:
+                transpose_x(*to_turn)
 
-            if i < UNITS:
-                q2 = act(three, "q2", a2[i], ACT.Square, b_col(2, i))
-            if 0 <= i - 2 < UNITS:
-                q1 = act(three, "q1", f1[i - 2], ACT.Square, 0.0)
-            if i < UNITS:
-                s2 = act(three, "s2", q2, ACT.Abs_reciprocal_sqrt, 0.5)
-            if 0 <= i - 2 < UNITS:
-                s1 = act(three, "s1", q1, ACT.Abs_reciprocal_sqrt, 0.5)
-            if i < UNITS:
-                w2t[i] = act(three, "w2t", s2, ACT.Square, 0.0)
-            if 0 <= i - 2 < UNITS:
-                w1t[i - 2] = act(three, "w1t", s1, ACT.Square, 0.0)
+            if new:
+                q2 = act("q2", a2[i], ACT.Square, b_col(2, i))
+            if i in (0, 1):
+                copy_w0(2 * i)
+            if low:
+                q1 = act("q1", f1[i - 2], ACT.Square, 0.0)
+            if new:
+                s2 = act("s2", q2, ACT.Abs_reciprocal_sqrt, 0.5)
+            if i in (0, 1):
+                copy_w0(2 * i + 1)
+            if low:
+                s1 = act("s1", q1, ACT.Abs_reciprocal_sqrt, 0.5)
+            if new:
+                w2t[i] = act("w2t", s2, ACT.Square, 0.0)
+            if low:
+                w1t[i - 2] = act("w1t", s1, ACT.Square, 0.0)
 
-            if 0 <= i - 3 < UNITS:
-                u = i - 3
-                r1[u] = two.tile([P, BLK], F32, name="r1")
-                nc.gpsimd.tensor_tensor(out=r1[u][:], in0=f1[u][:], in1=w1t[u][:], op=MULT)
-            hb, hp = divmod(i - 7, T)
-            if 0 <= hb < NB - 1:
-                gain_piece(nc.gpsimd, hb, hp, P)
+            if end:
+                r1[i - 3] = product(nc.gpsimd, two, "r1", f1[i - 3], w1t[i - 3])
+            if to_gain and not late:
+                gain_tile(nc.gpsimd, *to_gain)
 
-            if 0 <= i - 1 < UNITS:
+            if mid:
                 u = i - 1
-                r2[u] = two.tile([P, BLK], F32, name="r2")
+                r2[u] = two.tile([P, WIDTHS[u // T]], F32, name="r2")
                 nc.vector.scalar_tensor_tensor(
                     out=r2[u][:], in0=a2[u][:], scalar=b_col(2, u), in1=w2t[u][:], op0=ADD, op1=MULT
                 )
-            if k < 2 and nxt < NB:
-                scale_x_half(nxt, k)
-            if k == 2 and nxt < NB:
-                quantize_x(nxt)
-            if i == 0:
-                quantize_w(tw0, 0, L)
-            if i == 1:
-                quantize_w(tv, 0, O)
-            if 0 <= i - 1 < UNITS:
+            if to_scale and to_scale[0] > 0:
+                scale_x_tile(*to_scale)
+            if to_mix:
+                evict(nc.scalar.copy if i >= UNITS else nc.vector.tensor_copy, *to_mix)
+            if out_:
+                add_f0(i - 4)
+            if mid:
                 u = i - 1
-                f1[u] = four.tile([P, BLK], F32, name="f1")
+                f1[u] = four.tile([P, WIDTHS[u // T]], F32, name="f1")
                 nc.vector.scalar_tensor_tensor(
                     out=f1[u][:], in0=a1[u][:], scalar=b_col(1, u), in1=r2[u][:], op0=ADD, op1=ADD
                 )
-            if k == 3 and nxt + 1 < NB:
-                cast_x(nxt + 1)
-            ob, op = divmod(i - 9, T)
-            if 0 <= ob < NB - 1 and op in (0, 2):
-                quantize_h(ob, op // 2)
-                mix(ob, op // 2)
-            sb, sp = divmod(i - 10, T)
-            if 0 <= sb < NB - 1 and sp in (0, 2):
-                store(sb, sp // 2, nc.vector.tensor_copy)
-            if 0 <= i - 3 < UNITS:
-                u = i - 3
-                blk, t = divmod(u, T)
-                if t == 0:
-                    f0[blk] = three.tile([P, T, BLK], F32, name="f0")
-                nc.vector.scalar_tensor_tensor(
-                    out=f0[blk][:, t, :], in0=a0[u][:], scalar=b_col(0, u), in1=r1[u][:], op0=ADD, op1=ADD
+            if to_gain and late:
+                gain_tile(nc.vector, *to_gain)
+            if to_code:
+                quantize_h(to_code[0], to_code[1], to_code[1] + 1)
+            if to_cast and to_cast[0] > 0:
+                cast_x(nc.vector.tensor_copy, *to_cast)
+            if to_scale and to_scale[0] > 0:
+                quantize_x(to_scale[0], to_scale[1], to_scale[1] + 1)
+            if i == -3:
+                copy_w2(1)
+            if i == -2:
+                copy_w2(2)
+                quantize_w(tw2, P, 2 * P)
+            if i == -1:
+                copy_w2(3)
+                quantize_w(tw2, 2 * P, 3 * P)
+                quantize_w(tw1, 0, L)
+                quantize_w(tw2, 3 * P, L)
+            if i == 2:
+                quantize_w(tw0, 0, L)
+            if i == 4:
+                nc.vector.tensor_copy(
+                    out=tv[0][:].rearrange("p (c j) -> p c j", j=T), in_=raw_v[:].rearrange("p j c -> p c j")
                 )
+            if i == 5:
+                quantize_w(tv, 0, O)
 
         last, u = NB - 1, UNITS - 1
-        a0[u] = rung_matmul(p_a0, "a0", tw0, u)
-        gain_piece(nc.gpsimd, last - 1, T - 1, P)
-        store(last - 1, 0, nc.scalar.copy)
-        r1[u] = two.tile([P, BLK], F32, name="r1")
-        halves = (slice(0, 256), slice(256, 512))
-        for n in halves:
-            nc.vector.tensor_tensor(out=r1[u][:, n], in0=f1[u][:, n], in1=w1t[u][:, n], op=MULT)
-        for n in halves:
-            nc.vector.scalar_tensor_tensor(
-                out=f0[last][:, T - 1, n], in0=a0[u][:, n], scalar=b_col(0, u), in1=r1[u][:, n], op0=ADD, op1=ADD
-            )
-        quantize_h(last - 1, 1)
+        mix(last - 1, 0)
+        quantize_h(last - 1, 1, 2)
+        evict(nc.scalar.copy, last - 1, 0)
         mix(last - 1, 1)
-        store(last - 1, 1, nc.scalar.copy)
-        gain_piece(nc.vector, last, 0, 256)
-        gain_piece(nc.vector, last, 1, 256)
-        for half in range(2):
-            quantize_h(last, half)
-            mix(last, half)
-            store(last, half, nc.scalar.copy)
+        f0_matmul(u - 1)
+        gain_tile(nc.vector, last - 1, 2)
+        add_f0(u - 1)
+        evict(nc.scalar.copy, last - 1, 1)
+        gain_tile(nc.vector, last - 1, 3)
+        quantize_h(last - 1, 2, 3)
+        mix(last - 1, 2)
+        evict(nc.scalar.copy, last - 1, 2)
+        f0_matmul(u)
+        r1[u] = product(nc.vector, two, "r1", f1[u], w1t[u])
+        quantize_h(last - 1, 3, 4)
+        mix(last - 1, 3)
+        evict(nc.scalar.copy, last - 1, 3)
+        add_f0(u)
+        for r in range(2):
+            gain_tile(nc.vector, last, r)
+        for r in range(2):
+            quantize_h(last, r, r + 1)
+            mix(last, r)
+            evict(nc.scalar.copy, last, r)

@@ -22,6 +22,12 @@ WIDTHS = (256, 512, 512, 512, 512, 512, 512, 512, 256)
 NB = len(WIDTHS)
 STARTS = tuple(sum(WIDTHS[:i]) for i in range(NB))
 UNITS = NB * T
+GAIN_V = (24, 28, 29, 30, 31, 32, 34)
+F0AT = 0
+R1_V = ()
+W2_G = range(0, 32)
+SPLIT = 96
+Q0_AT = 3
 
 
 def tile_cofrnetladderlayer_t_kernel(tc, x_bytes, x_scale, w0, w1, w2, b, g, v, out):
@@ -36,7 +42,7 @@ def tile_cofrnetladderlayer_t_kernel(tc, x_bytes, x_scale, w0, w1, w2, b, g, v, 
         p_a1 = ctx.enter_context(tc.psum_pool(name="p_a1", bufs=1))
         p_a0 = ctx.enter_context(tc.psum_pool(name="p_a0", bufs=1))
         p_xt = ctx.enter_context(tc.psum_pool(name="p_xt", bufs=2))
-        p_out = ctx.enter_context(tc.psum_pool(name="p_out", bufs=1))
+        p_out = ctx.enter_context(tc.psum_pool(name="p_out", bufs=4 - 3))
         ctx.enter_context(tc.manual_schedule())
 
         x8 = {}
@@ -53,8 +59,8 @@ def tile_cofrnetladderlayer_t_kernel(tc, x_bytes, x_scale, w0, w1, w2, b, g, v, 
             return raw
 
         load_x(0)
-        raw2 = load_w(w2, "w2")
         raw1 = load_w(w1, "w1")
+        raw2 = load_w(w2, "w2")
         load_x(1)
         raw0 = load_w(w0, "w0")
         load_x(2)
@@ -138,8 +144,11 @@ def tile_cofrnetladderlayer_t_kernel(tc, x_bytes, x_scale, w0, w1, w2, b, g, v, 
         def copy_w2(t):
             nc.vector.tensor_copy(out=grouped(tw2)[:, t], in_=permuted(raw2)[:, t])
 
-        def copy_w0(t):
-            nc.scalar.copy(out=grouped(tw0)[:, t], in_=permuted(raw0)[:, t])
+        def regroup(copy, tiles, raw, t):
+            copy(out=grouped(tiles)[:, t], in_=permuted(raw)[:, t])
+
+        def regroup_by_gpsimd(out, in_):
+            nc.gpsimd.tensor_scalar(out=out, in0=in_, scalar1=1.0, scalar2=0.0, op0=MULT, op1=ADD)
 
         a2, a1, a0 = {}, {}, {}
         w2t, r2, f1, w1t, r1, f0 = {}, {}, {}, {}, {}, {}
@@ -224,24 +233,26 @@ def tile_cofrnetladderlayer_t_kernel(tc, x_bytes, x_scale, w0, w1, w2, b, g, v, 
             if not 0 <= blk < NB:
                 return None
             every = T * P // WIDTHS[blk]
-            return (blk, k // every) if k % every == 0 else None
+            return (blk, k // every) if k % every == 0 and k // every < WIDTHS[blk] // P else None
 
         cast_x(nc.vector.tensor_copy, 0, 0)
         cast_x(nc.scalar.copy, 0, 1)
         transpose_x(0, 0)
         transpose_x(0, 1)
         nc.scalar.copy(out=grouped(tw1), in_=permuted(raw1))
-        copy_w2(0)
         scale_x_tile(0, 0)
-        quantize_w(tw2, 0, P)
         scale_x_tile(0, 1)
         bias = keep.tile([P, 3, T], F32, name="bias")
         nc.vector.tensor_copy(out=bias[:], in_=b_raw[:])
         gain = keep.tile([P, T], F32, name="gain")
         nc.vector.tensor_copy(out=gain[:], in_=g_raw[:])
+        copy_w2(0)
         quantize_x(0, 0, 2)
+        quantize_w(tw2, 0, P)
         a2[0] = rung_matmul(p_a2, "a2", tw2, 0)
 
+        SA = {0: (tw0, raw0, 0), 1: (tw0, raw0, 2)}
+        SB = {0: (tw0, raw0, 1), 1: (tw0, raw0, 3)}
         def f0_matmul(u):
             a0[u] = rung_matmul(p_a0, "a0", tw0, u)
 
@@ -259,7 +270,6 @@ def tile_cofrnetladderlayer_t_kernel(tc, x_bytes, x_scale, w0, w1, w2, b, g, v, 
             low = 0 <= i - 2 < UNITS
             end = 0 <= i - 3 < UNITS
             out_ = 0 <= i - 4 < UNITS
-            late = i >= UNITS - 6
             to_cast = tile_at(i + 7)
             to_turn = tile_at(i + 6)
             to_scale = tile_at(i + 5)
@@ -267,38 +277,42 @@ def tile_cofrnetladderlayer_t_kernel(tc, x_bytes, x_scale, w0, w1, w2, b, g, v, 
             to_code = tile_at(i - 9)
             to_mix = tile_at(i - 10)
 
-            if mid:
-                a1[i - 1] = rung_matmul(p_a1, "a1", tw1, i - 1)
             if out_:
                 f0_matmul(i - 4)
-            if to_mix:
-                mix(*to_mix)
-            if 0 <= i and i + 1 < UNITS:
-                a2[i + 1] = rung_matmul(p_a2, "a2", tw2, i + 1)
+            if mid:
+                a1[i - 1] = rung_matmul(p_a1, "a1", tw1, i - 1)
             if to_turn and to_turn[0] > 0:
                 transpose_x(*to_turn)
+            if 0 <= i and i + 1 < UNITS:
+                a2[i + 1] = rung_matmul(p_a2, "a2", tw2, i + 1)
+            if to_mix:
+                mix(*to_mix)
 
             if new:
                 q2 = act("q2", a2[i], ACT.Square, b_col(2, i))
-            if i in (0, 1):
-                copy_w0(2 * i)
+            if i in SA:
+                regroup(nc.scalar.copy, *SA[i])
             if low:
                 q1 = act("q1", f1[i - 2], ACT.Square, 0.0)
             if new:
                 s2 = act("s2", q2, ACT.Abs_reciprocal_sqrt, 0.5)
-            if i in (0, 1):
-                copy_w0(2 * i + 1)
+            if i in SB:
+                regroup(nc.scalar.copy, *SB[i])
             if low:
                 s1 = act("s1", q1, ACT.Abs_reciprocal_sqrt, 0.5)
             if new:
-                w2t[i] = act("w2t", s2, ACT.Square, 0.0)
+                cut = WIDTHS[i // T] - (SPLIT if i in W2_G else 0)
+                w2t[i] = three.tile([P, WIDTHS[i // T]], F32, name="w2t")
+                nc.scalar.activation(out=w2t[i][:, :cut], in_=s2[:, :cut], func=ACT.Square)
             if low:
                 w1t[i - 2] = act("w1t", s1, ACT.Square, 0.0)
 
             if end:
-                r1[i - 3] = product(nc.gpsimd, two, "r1", f1[i - 3], w1t[i - 3])
-            if to_gain and not late:
+                r1[i - 3] = product(nc.vector if i - 3 in R1_V else nc.gpsimd, two, "r1", f1[i - 3], w1t[i - 3])
+            if to_gain and i - 8 not in GAIN_V:
                 gain_tile(nc.gpsimd, *to_gain)
+            if new and i in W2_G:
+                nc.gpsimd.tensor_tensor(out=w2t[i][:, cut:], in0=s2[:, cut:], in1=s2[:, cut:], op=MULT)
 
             if mid:
                 u = i - 1
@@ -308,8 +322,6 @@ def tile_cofrnetladderlayer_t_kernel(tc, x_bytes, x_scale, w0, w1, w2, b, g, v, 
                 )
             if to_scale and to_scale[0] > 0:
                 scale_x_tile(*to_scale)
-            if to_mix:
-                evict(nc.scalar.copy if i >= UNITS else nc.vector.tensor_copy, *to_mix)
             if out_:
                 add_f0(i - 4)
             if mid:
@@ -318,12 +330,14 @@ def tile_cofrnetladderlayer_t_kernel(tc, x_bytes, x_scale, w0, w1, w2, b, g, v, 
                 nc.vector.scalar_tensor_tensor(
                     out=f1[u][:], in0=a1[u][:], scalar=b_col(1, u), in1=r2[u][:], op0=ADD, op1=ADD
                 )
-            if to_gain and late:
+            if to_cast and to_cast[0] > 0:
+                cast_x(nc.vector.tensor_copy, *to_cast)
+            if to_mix:
+                evict(nc.scalar.copy if i >= UNITS else nc.vector.tensor_copy, *to_mix)
+            if to_gain and i - 8 in GAIN_V:
                 gain_tile(nc.vector, *to_gain)
             if to_code:
                 quantize_h(to_code[0], to_code[1], to_code[1] + 1)
-            if to_cast and to_cast[0] > 0:
-                cast_x(nc.vector.tensor_copy, *to_cast)
             if to_scale and to_scale[0] > 0:
                 quantize_x(to_scale[0], to_scale[1], to_scale[1] + 1)
             if i == -3:
@@ -336,7 +350,7 @@ def tile_cofrnetladderlayer_t_kernel(tc, x_bytes, x_scale, w0, w1, w2, b, g, v, 
                 quantize_w(tw2, 2 * P, 3 * P)
                 quantize_w(tw1, 0, L)
                 quantize_w(tw2, 3 * P, L)
-            if i == 2:
+            if i == Q0_AT:
                 quantize_w(tw0, 0, L)
             if i == 4:
                 nc.vector.tensor_copy(
@@ -346,27 +360,26 @@ def tile_cofrnetladderlayer_t_kernel(tc, x_bytes, x_scale, w0, w1, w2, b, g, v, 
                 quantize_w(tv, 0, O)
 
         last, u = NB - 1, UNITS - 1
-        mix(last - 1, 0)
-        quantize_h(last - 1, 1, 2)
-        evict(nc.scalar.copy, last - 1, 0)
-        mix(last - 1, 1)
+        before = [t for t in (tile_at(s) for s in range(UNITS - 8, UNITS - 4)) if t]
+        final = [t for t in (tile_at(s) for s in range(UNITS - 4, UNITS)) if t]
+        gains = [t for t in (tile_at(s) for s in range(UNITS - 6, UNITS - 4)) if t]
+        codes = [t for t in (tile_at(s) for s in range(UNITS - 7, UNITS - 4)) if t]
         f0_matmul(u - 1)
-        gain_tile(nc.vector, last - 1, 2)
-        add_f0(u - 1)
-        evict(nc.scalar.copy, last - 1, 1)
-        gain_tile(nc.vector, last - 1, 3)
-        quantize_h(last - 1, 2, 3)
-        mix(last - 1, 2)
-        evict(nc.scalar.copy, last - 1, 2)
-        f0_matmul(u)
+        for t in before:
+            if t in gains:
+                gain_tile(nc.vector if UNITS - 8 + t[1] in GAIN_V else nc.gpsimd, *t)
+            if t in codes:
+                quantize_h(t[0], t[1], t[1] + 1)
+            mix(*t)
+            evict(nc.scalar.copy, *t)
+            if t == before[F0AT]:
+                add_f0(u - 1)
+                f0_matmul(u)
         r1[u] = product(nc.vector, two, "r1", f1[u], w1t[u])
-        quantize_h(last - 1, 3, 4)
-        mix(last - 1, 3)
-        evict(nc.scalar.copy, last - 1, 3)
         add_f0(u)
-        for r in range(2):
-            gain_tile(nc.vector, last, r)
-        for r in range(2):
-            quantize_h(last, r, r + 1)
-            mix(last, r)
-            evict(nc.scalar.copy, last, r)
+        for t in final:
+            gain_tile(nc.vector if UNITS - 4 + 2 * t[1] in GAIN_V else nc.gpsimd, *t)
+        for t in final:
+            quantize_h(t[0], t[1], t[1] + 1)
+            mix(*t)
+            evict(nc.scalar.copy, *t)

@@ -18,368 +18,395 @@ ACT = mybir.ActivationFunctionType
 
 P = 128
 T = 4
+
 WIDTHS = (256, 512, 512, 512, 512, 512, 512, 512, 256)
-NB = len(WIDTHS)
-STARTS = tuple(sum(WIDTHS[:i]) for i in range(NB))
-UNITS = NB * T
-GAIN_V = (24, 28, 29, 30, 31, 32, 34)
-F0AT = 0
-R1_V = ()
-W2_G = range(0, 32)
-SPLIT = 96
-Q0_AT = 3
+BLOCKS = len(WIDTHS)
+STARTS = tuple(sum(WIDTHS[:i]) for i in range(BLOCKS))
+UNITS = BLOCKS * T
+
+GPSIMD_COLUMNS = 96
+
+
+def gain_on_vector(step):
+    return step >= UNITS - 2 * T or step == UNITS - 3 * T
+
+
+def token_tile_at(step):
+    block, k = divmod(step, T)
+    if not 0 <= block < BLOCKS:
+        return None
+    every = T * P // WIDTHS[block]
+    return (block, k // every) if k % every == 0 else None
 
 
 def tile_cofrnetladderlayer_t_kernel(tc, x_bytes, x_scale, w0, w1, w2, b, g, v, out):
     nc = tc.nc
     with ExitStack() as ctx:
         keep = ctx.enter_context(tc.tile_pool(name="keep", bufs=1))
-        xin = ctx.enter_context(tc.tile_pool(name="xin", bufs=NB))
-        two = ctx.enter_context(tc.tile_pool(name="two", bufs=3))
-        three = ctx.enter_context(tc.tile_pool(name="three", bufs=4))
-        four = ctx.enter_context(tc.tile_pool(name="four", bufs=5))
+        x_in = ctx.enter_context(tc.tile_pool(name="x_in", bufs=BLOCKS))
+        three = ctx.enter_context(tc.tile_pool(name="three", bufs=3))
+        four = ctx.enter_context(tc.tile_pool(name="four", bufs=4))
+        five = ctx.enter_context(tc.tile_pool(name="five", bufs=5))
         p_a2 = ctx.enter_context(tc.psum_pool(name="p_a2", bufs=3))
         p_a1 = ctx.enter_context(tc.psum_pool(name="p_a1", bufs=1))
         p_a0 = ctx.enter_context(tc.psum_pool(name="p_a0", bufs=1))
         p_xt = ctx.enter_context(tc.psum_pool(name="p_xt", bufs=2))
-        p_out = ctx.enter_context(tc.psum_pool(name="p_out", bufs=4 - 3))
+        p_out = ctx.enter_context(tc.psum_pool(name="p_out", bufs=1))
         ctx.enter_context(tc.manual_schedule())
 
         x8 = {}
 
-        def load_x(blk):
-            width = WIDTHS[blk]
-            x8[blk] = xin.tile([P, width // P, D], U8, name="x8")
-            rows = x_bytes[STARTS[blk] : STARTS[blk] + width, :]
-            nc.sync.dma_start(out=x8[blk][:], in_=rows.rearrange("(p r) k -> p r k", p=P))
+        def load_x(block):
+            width = WIDTHS[block]
+            x8[block] = x_in.tile([P, width // P, D], U8, name="x8")
+            rows = x_bytes[STARTS[block] : STARTS[block] + width, :]
+            nc.sync.dma_start(out=x8[block][:], in_=rows.rearrange("(p r) k -> p r k", p=P))
 
-        def load_w(w, name):
+        def load_weights(w, name):
             raw = keep.tile([P, T, w.shape[1]], BF16, name="raw_" + name)
             nc.sync.dma_start(out=raw[:], in_=w.rearrange("(p j) c -> p j c", j=T))
             return raw
 
         load_x(0)
-        raw1 = load_w(w1, "w1")
-        raw2 = load_w(w2, "w2")
+        raw_w1 = load_weights(w1, "w1")
+        raw_w2 = load_weights(w2, "w2")
         load_x(1)
-        raw0 = load_w(w0, "w0")
+        raw_w0 = load_weights(w0, "w0")
         load_x(2)
-        raw_v = load_w(v, "v")
-        for blk in range(3, NB):
-            load_x(blk)
+        raw_v = load_weights(v, "v")
+        for block in range(3, BLOCKS):
+            load_x(block)
 
         scale_x = keep.tile([P, T], F32, name="scale_x")
         nc.scalar.dma_start(out=scale_x[:], in_=x_scale.rearrange("o (p t) -> p (o t)", t=T))
-        b_raw = keep.tile([P, 3, T], BF16, name="b_raw")
-        nc.scalar.dma_start(out=b_raw[:], in_=b.rearrange("i (p t) -> p i t", t=T))
-        g_raw = keep.tile([P, T], BF16, name="g_raw")
-        nc.scalar.dma_start(out=g_raw[:], in_=g.rearrange("(p t) -> p t", t=T))
+        raw_b = keep.tile([P, 3, T], BF16, name="raw_b")
+        nc.scalar.dma_start(out=raw_b[:], in_=b.rearrange("i (p t) -> p i t", t=T))
+        raw_g = keep.tile([P, T], BF16, name="raw_g")
+        nc.scalar.dma_start(out=raw_g[:], in_=g.rearrange("(p t) -> p t", t=T))
 
-        ident = keep.tile([P, P], F32, name="ident")
-        make_identity(nc, ident[:])
+        identity = keep.tile([P, P], F32, name="identity")
+        make_identity(nc, identity[:])
 
-        warm = keep.tile([P, 1], F32, name="warm")
-        nc.vector.memset(warm[:], 1.0)
+        warm_in = keep.tile([P, 1], F32, name="warm_in")
+        nc.vector.memset(warm_in[:], 1.0)
         warm_out = keep.tile([P, 1], F32, name="warm_out")
-        nc.scalar.activation(out=warm_out[:], in_=warm[:], func=ACT.Abs_reciprocal_sqrt)
+        nc.scalar.activation(out=warm_out[:], in_=warm_in[:], func=ACT.Abs_reciprocal_sqrt)
 
-        xb, xt, xs, xq, xqs = {}, {}, {}, {}, {}
+        bias = keep.tile([P, 3, T], F32, name="bias")
+        gain = keep.tile([P, T], F32, name="gain")
 
-        def cast_x(copy, blk, r):
+        x_rows, x_turned, x_bf16, x_codes, x_scales = {}, {}, {}, {}, {}
+
+        def widen_x(copy, block, r):
             if r == 0:
-                xb[blk] = two.tile([P, WIDTHS[blk] // P, D], BF16, name="xb")
-            copy(out=xb[blk][:, r, :], in_=x8[blk][:, r, :].bitcast(FP8))
+                x_rows[block] = three.tile([P, WIDTHS[block] // P, D], BF16, name="x_rows")
+            copy(out=x_rows[block][:, r, :], in_=x8[block][:, r, :].bitcast(FP8))
 
-        def transpose_x(blk, r):
-            words = xb[blk][:].bitcast(F32)
-            xt[blk, r] = p_xt.tile([P, 2, P], F32, name="xt")
+        def turn_x(block, r):
+            words = x_rows[block][:].bitcast(F32)
+            x_turned[block, r] = p_xt.tile([P, 2, P], F32, name="xt")
             for u in range(2):
-                nc.tensor.transpose(xt[blk, r][:, u, :], words[:, r, u : D // 2 : 2], ident[:])
+                nc.tensor.transpose(x_turned[block, r][:, u, :], words[:, r, u : D // 2 : 2], identity[:])
 
-        def scale_x_tile(blk, r):
+        def scale_x_tile(block, r):
             if r == 0:
-                xs[blk] = two.tile([P, WIDTHS[blk], T], BF16, name="xs", align_bytes=64)
+                x_bf16[block] = three.tile([P, WIDTHS[block], T], BF16, name="x_bf16", align_bytes=64)
             nc.vector.tensor_tensor(
-                out=xs[blk][:, r * P : (r + 1) * P, :].rearrange("p m (u e) -> p m u e", e=2),
-                in0=xt[blk, r][:].bitcast(BF16).rearrange("p u (m e) -> p m u e", e=2),
+                out=x_bf16[block][:, r * P : (r + 1) * P, :].rearrange("p m (u e) -> p m u e", e=2),
+                in0=x_turned[block, r][:].bitcast(BF16).rearrange("p u (m e) -> p m u e", e=2),
                 in1=scale_x[:].unsqueeze(1).to_broadcast([P, P, T]).rearrange("p m (u e) -> p m u e", e=2),
                 op=MULT,
             )
 
-        def quantize_x(blk, r0, r1):
+        def quantize_x(block, r0, r1):
             if r0 == 0:
-                xq[blk] = three.tile([P, WIDTHS[blk]], U32, name="xq", align_bytes=64)
-                xqs[blk] = three.tile([P, WIDTHS[blk]], U8, name="xqs", align_bytes=64)
+                x_codes[block] = four.tile([P, WIDTHS[block]], U32, name="x_codes", align_bytes=64)
+                x_scales[block] = four.tile([P, WIDTHS[block]], U8, name="x_scales", align_bytes=64)
             n = slice(r0 * P, r1 * P)
             nc.vector.quantize_mx(
-                out=xq[blk][:, n].bitcast(FP8X4),
-                scales=xqs[blk][:, n],
-                in_=xs[blk][:, n, :].rearrange("p m t -> p (m t)"),
+                out=x_codes[block][:, n].bitcast(FP8X4),
+                scales=x_scales[block][:, n],
+                in_=x_bf16[block][:, n, :].rearrange("p m t -> p (m t)"),
             )
 
         def weight_tiles(name, width):
             return (
-                keep.tile([P, T * width], BF16, name="grp_" + name, align_bytes=64),
-                keep.tile([P, width], U32, name="cod_" + name, align_bytes=64),
-                keep.tile([P, width], U8, name="sca_" + name, align_bytes=64),
+                keep.tile([P, T * width], BF16, name="bf16_" + name, align_bytes=64),
+                keep.tile([P, width], U32, name="codes_" + name, align_bytes=64),
+                keep.tile([P, width], U8, name="scales_" + name, align_bytes=64),
             )
 
-        def quantize_w(tiles, c0, c1):
-            grp, cod, sca = tiles
-            nc.vector.quantize_mx(
-                out=cod[:, c0:c1].bitcast(FP8X4), scales=sca[:, c0:c1], in_=grp[:, T * c0 : T * c1]
-            )
+        weights2 = weight_tiles("w2", L)
+        weights1 = weight_tiles("w1", L)
+        weights0 = weight_tiles("w0", L)
+        weights_v = weight_tiles("v", O)
 
-        tw2 = weight_tiles("w2", L)
-        tw1 = weight_tiles("w1", L)
-        tw0 = weight_tiles("w0", L)
-        tv = weight_tiles("v", O)
-
-        def permuted(raw):
+        def by_channel(raw):
             return raw[:].rearrange("p j (m t) -> p t m j", t=T)
 
         def grouped(tiles):
             return tiles[0][:].rearrange("p (t m j) -> p t m j", t=T, j=T)
 
-        def copy_w2(t):
-            nc.vector.tensor_copy(out=grouped(tw2)[:, t], in_=permuted(raw2)[:, t])
+        def group(copy, tiles, raw, t):
+            copy(out=grouped(tiles)[:, t], in_=by_channel(raw)[:, t])
 
-        def regroup(copy, tiles, raw, t):
-            copy(out=grouped(tiles)[:, t], in_=permuted(raw)[:, t])
-
-        def regroup_by_gpsimd(out, in_):
-            nc.gpsimd.tensor_scalar(out=out, in0=in_, scalar1=1.0, scalar2=0.0, op0=MULT, op1=ADD)
+        def quantize_weights(tiles, c0, c1):
+            bf16, codes, scales = tiles
+            nc.vector.quantize_mx(
+                out=codes[:, c0:c1].bitcast(FP8X4), scales=scales[:, c0:c1], in_=bf16[:, T * c0 : T * c1]
+            )
 
         a2, a1, a0 = {}, {}, {}
-        w2t, r2, f1, w1t, r1, f0 = {}, {}, {}, {}, {}, {}
+        w_rung2, w_rung1 = {}, {}
+        r2, f1, r1, f0 = {}, {}, {}, {}
 
-        def rung_matmul(pool, name, tiles, u):
-            blk, t = divmod(u, T)
-            bank = pool.tile([P, WIDTHS[blk]], F32, name=name)
-            cols = slice(t * P, (t + 1) * P)
+        def multiply_x(pool, name, tiles, unit):
+            block, t = divmod(unit, T)
+            bank = pool.tile([P, WIDTHS[block]], F32, name=name)
+            channels = slice(t * P, (t + 1) * P)
             nc.tensor.matmul_mx(
                 out=bank[:],
-                lhsT=tiles[1][:, cols].bitcast(FP8X4),
-                lhsT_scale=tiles[2][:, cols],
-                rhs=xq[blk][:].bitcast(FP8X4),
-                rhs_scale=xqs[blk][:],
+                lhsT=tiles[1][:, channels].bitcast(FP8X4),
+                lhsT_scale=tiles[2][:, channels],
+                rhs=x_codes[block][:].bitcast(FP8X4),
+                rhs_scale=x_scales[block][:],
                 start=True,
                 stop=True,
             )
             return bank
 
-        def b_col(i, u):
-            t = u % T
-            return bias[:, i, t : t + 1]
+        def bias_of(rung, unit):
+            t = unit % T
+            return bias[:, rung, t : t + 1]
 
-        def act(name, src, func, bias_in):
-            dst = three.tile([P, src.shape[1]], F32, name=name)
+        def activate(name, src, func, bias_in):
+            dst = four.tile([P, src.shape[1]], F32, name=name)
             nc.scalar.activation(out=dst[:], in_=src[:], func=func, bias=bias_in)
             return dst
 
-        def product(eng, pool, name, a, c):
-            dst = pool.tile([P, a.shape[1]], F32, name=name)
-            eng.tensor_tensor(out=dst[:], in0=a[:], in1=c[:], op=MULT)
-            return dst
+        def multiply_r1(eng, unit):
+            r1[unit] = three.tile([P, WIDTHS[unit // T]], F32, name="r1")
+            eng.tensor_tensor(out=r1[unit][:], in0=f1[unit][:], in1=w_rung1[unit][:], op=MULT)
 
-        hh, hq, hqs, po, osb = {}, {}, {}, {}, {}
+        def multiply_a0(unit):
+            a0[unit] = multiply_x(p_a0, "a0", weights0, unit)
 
-        def gain_tile(eng, blk, r):
+        def add_f0(unit):
+            block, t = divmod(unit, T)
+            if t == 0:
+                f0[block] = three.tile([P, T, WIDTHS[block]], F32, name="f0")
+            nc.vector.scalar_tensor_tensor(
+                out=f0[block][:, t, :],
+                in0=a0[unit][:],
+                scalar=bias_of(0, unit),
+                in1=r1[unit][:],
+                op0=ADD,
+                op1=ADD,
+            )
+
+        h_bf16, h_codes, h_scales, mixed, out_rows = {}, {}, {}, {}, {}
+
+        def gain_tile(eng, block, r):
             if r == 0:
-                hh[blk] = two.tile([P, WIDTHS[blk], T], BF16, name="hh", align_bytes=64)
+                h_bf16[block] = three.tile([P, WIDTHS[block], T], BF16, name="h_bf16", align_bytes=64)
             n = slice(r * P, (r + 1) * P)
             eng.tensor_tensor(
-                out=hh[blk][:, n, :].rearrange("p (c i) t -> p c t i", i=4),
-                in0=f0[blk][:, :, n].rearrange("p t (c i) -> p c t i", i=4),
+                out=h_bf16[block][:, n, :].rearrange("p (c i) t -> p c t i", i=4),
+                in0=f0[block][:, :, n].rearrange("p t (c i) -> p c t i", i=4),
                 in1=gain[:].unsqueeze(1).unsqueeze(3).to_broadcast([P, P // 4, T, 4]),
                 op=MULT,
             )
 
-        def quantize_h(blk, r0, r1):
-            if r0 == 0:
-                hq[blk] = two.tile([P, WIDTHS[blk]], U32, name="hq", align_bytes=64)
-                hqs[blk] = two.tile([P, WIDTHS[blk]], U8, name="hqs", align_bytes=64)
-            n = slice(r0 * P, r1 * P)
+        def gain_tile_by_scalar(block, r):
+            n = slice(r * P, (r + 1) * P)
+            for t in range(T):
+                nc.scalar.activation(
+                    out=h_bf16[block][:, n, t], in_=f0[block][:, t, n], func=ACT.Copy, scale=gain[:, t : t + 1]
+                )
+
+        def quantize_h(block, r):
+            if r == 0:
+                h_codes[block] = three.tile([P, WIDTHS[block]], U32, name="h_codes", align_bytes=64)
+                h_scales[block] = three.tile([P, WIDTHS[block]], U8, name="h_scales", align_bytes=64)
+            n = slice(r * P, (r + 1) * P)
             nc.vector.quantize_mx(
-                out=hq[blk][:, n].bitcast(FP8X4),
-                scales=hqs[blk][:, n],
-                in_=hh[blk][:, n, :].rearrange("p m t -> p (m t)"),
+                out=h_codes[block][:, n].bitcast(FP8X4),
+                scales=h_scales[block][:, n],
+                in_=h_bf16[block][:, n, :].rearrange("p m t -> p (m t)"),
             )
 
-        def mix(blk, r):
-            po[blk, r] = p_out.tile([P, O], F32, name="po")
-            rows = slice(r * P, (r + 1) * P)
+        def mix_into(bank, block, r):
+            mixed[block, r] = bank
+            tokens = slice(r * P, (r + 1) * P)
             nc.tensor.matmul_mx(
-                out=po[blk, r][:],
-                lhsT=hq[blk][:, rows].bitcast(FP8X4),
-                lhsT_scale=hqs[blk][:, rows],
-                rhs=tv[1][:].bitcast(FP8X4),
-                rhs_scale=tv[2][:],
+                out=bank[:],
+                lhsT=h_codes[block][:, tokens].bitcast(FP8X4),
+                lhsT_scale=h_scales[block][:, tokens],
+                rhs=weights_v[1][:].bitcast(FP8X4),
+                rhs_scale=weights_v[2][:],
                 start=True,
                 stop=True,
             )
 
-        def evict(copy, blk, r):
-            tiles = WIDTHS[blk] // P
+        def mix(block, r):
+            bank = p_out.tile([P, O], F32, name="mixed")
+            mix_into(bank, block, r)
+
+        def mix_in_x_bank(block, r):
+            bank = p_xt.tile([P, O], F32, name="xt")
+            mix_into(bank, block, r)
+
+        def store(copy, block, r):
             if r == 0:
-                osb[blk] = three.tile([P, tiles, O], F32, name="osb")
-            copy(out=osb[blk][:, r, :], in_=po[blk, r][:])
-            if r == tiles - 1:
-                dst = out[STARTS[blk] : STARTS[blk] + WIDTHS[blk], :].rearrange("(p r) o -> p r o", p=P)
-                nc.sync.dma_start(out=dst, in_=osb[blk][:])
+                out_rows[block] = four.tile([P, WIDTHS[block] // P, O], F32, name="out_rows")
+            copy(out=out_rows[block][:, r, :], in_=mixed[block, r][:])
+            if r % 2 == 1:
+                rows = out[STARTS[block] : STARTS[block] + WIDTHS[block], :].rearrange("(p r) o -> p r o", p=P)
+                nc.sync.dma_start(out=rows[:, r - 1 : r + 1, :], in_=out_rows[block][:, r - 1 : r + 1, :])
 
-        def tile_at(step):
-            blk, k = divmod(step, T)
-            if not 0 <= blk < NB:
-                return None
-            every = T * P // WIDTHS[blk]
-            return (blk, k // every) if k % every == 0 and k // every < WIDTHS[blk] // P else None
-
-        cast_x(nc.vector.tensor_copy, 0, 0)
-        cast_x(nc.scalar.copy, 0, 1)
-        transpose_x(0, 0)
-        transpose_x(0, 1)
-        nc.scalar.copy(out=grouped(tw1), in_=permuted(raw1))
+        widen_x(nc.vector.tensor_copy, 0, 0)
+        widen_x(nc.scalar.copy, 0, 1)
+        turn_x(0, 0)
+        turn_x(0, 1)
+        nc.scalar.copy(out=grouped(weights1), in_=by_channel(raw_w1))
         scale_x_tile(0, 0)
         scale_x_tile(0, 1)
-        bias = keep.tile([P, 3, T], F32, name="bias")
-        nc.vector.tensor_copy(out=bias[:], in_=b_raw[:])
-        gain = keep.tile([P, T], F32, name="gain")
-        nc.vector.tensor_copy(out=gain[:], in_=g_raw[:])
-        copy_w2(0)
+        nc.vector.tensor_copy(out=bias[:], in_=raw_b[:])
+        nc.vector.tensor_copy(out=gain[:], in_=raw_g[:])
+        group(nc.vector.tensor_copy, weights2, raw_w2, 0)
         quantize_x(0, 0, 2)
-        quantize_w(tw2, 0, P)
-        a2[0] = rung_matmul(p_a2, "a2", tw2, 0)
-
-        SA = {0: (tw0, raw0, 0), 1: (tw0, raw0, 2)}
-        SB = {0: (tw0, raw0, 1), 1: (tw0, raw0, 3)}
-        def f0_matmul(u):
-            a0[u] = rung_matmul(p_a0, "a0", tw0, u)
-
-        def add_f0(u):
-            blk, t = divmod(u, T)
-            if t == 0:
-                f0[blk] = two.tile([P, T, WIDTHS[blk]], F32, name="f0")
-            nc.vector.scalar_tensor_tensor(
-                out=f0[blk][:, t, :], in0=a0[u][:], scalar=b_col(0, u), in1=r1[u][:], op0=ADD, op1=ADD
-            )
+        quantize_weights(weights2, 0, P)
+        a2[0] = multiply_x(p_a2, "a2", weights2, 0)
 
         for i in range(-3, UNITS + 2):
-            new = 0 <= i < UNITS
-            mid = 0 <= i - 1 < UNITS
-            low = 0 <= i - 2 < UNITS
-            end = 0 <= i - 3 < UNITS
-            out_ = 0 <= i - 4 < UNITS
-            to_cast = tile_at(i + 7)
-            to_turn = tile_at(i + 6)
-            to_scale = tile_at(i + 5)
-            to_gain = tile_at(i - 8)
-            to_code = tile_at(i - 9)
-            to_mix = tile_at(i - 10)
+            rung2_now = 0 <= i < UNITS
+            f1_now = 0 <= i - 1 < UNITS
+            rung1_now = 0 <= i - 2 < UNITS
+            r1_now = 0 <= i - 3 < UNITS
+            f0_now = 0 <= i - 4 < UNITS
+            to_widen, to_turn, to_scale = (t if t and t[0] > 0 else None for t in map(token_tile_at, (i + 7, i + 6, i + 5)))
+            to_gain, to_quantize, to_mix = map(token_tile_at, (i - 8, i - 9, i - 10))
 
-            if out_:
-                f0_matmul(i - 4)
-            if mid:
-                a1[i - 1] = rung_matmul(p_a1, "a1", tw1, i - 1)
-            if to_turn and to_turn[0] > 0:
-                transpose_x(*to_turn)
-            if 0 <= i and i + 1 < UNITS:
-                a2[i + 1] = rung_matmul(p_a2, "a2", tw2, i + 1)
+            if f0_now:
+                multiply_a0(i - 4)
+            if f1_now:
+                a1[i - 1] = multiply_x(p_a1, "a1", weights1, i - 1)
+            if to_turn:
+                turn_x(*to_turn)
+            if 0 <= i < UNITS - 1:
+                a2[i + 1] = multiply_x(p_a2, "a2", weights2, i + 1)
             if to_mix:
                 mix(*to_mix)
 
-            if new:
-                q2 = act("q2", a2[i], ACT.Square, b_col(2, i))
-            if i in SA:
-                regroup(nc.scalar.copy, *SA[i])
-            if low:
-                q1 = act("q1", f1[i - 2], ACT.Square, 0.0)
-            if new:
-                s2 = act("s2", q2, ACT.Abs_reciprocal_sqrt, 0.5)
-            if i in SB:
-                regroup(nc.scalar.copy, *SB[i])
-            if low:
-                s1 = act("s1", q1, ACT.Abs_reciprocal_sqrt, 0.5)
-            if new:
-                cut = WIDTHS[i // T] - (SPLIT if i in W2_G else 0)
-                w2t[i] = three.tile([P, WIDTHS[i // T]], F32, name="w2t")
-                nc.scalar.activation(out=w2t[i][:, :cut], in_=s2[:, :cut], func=ACT.Square)
-            if low:
-                w1t[i - 2] = act("w1t", s1, ACT.Square, 0.0)
+            if rung2_now:
+                q2 = activate("q2", a2[i], ACT.Square, bias_of(2, i))
+            if i in (0, 1):
+                group(nc.scalar.copy, weights0, raw_w0, 2 * i)
+            if rung1_now:
+                q1 = activate("q1", f1[i - 2], ACT.Square, 0.0)
+            if rung2_now:
+                s2 = activate("s2", q2, ACT.Abs_reciprocal_sqrt, 0.5)
+            if i in (0, 1):
+                group(nc.scalar.copy, weights0, raw_w0, 2 * i + 1)
+            if rung1_now:
+                s1 = activate("s1", q1, ACT.Abs_reciprocal_sqrt, 0.5)
+            if rung2_now:
+                width = WIDTHS[i // T]
+                cut = width - GPSIMD_COLUMNS if i < UNITS - T else width
+                w_rung2[i] = four.tile([P, width], F32, name="w_rung2")
+                nc.scalar.activation(out=w_rung2[i][:, :cut], in_=s2[:, :cut], func=ACT.Square)
+            if rung1_now:
+                w_rung1[i - 2] = activate("w_rung1", s1, ACT.Square, 0.0)
 
-            if end:
-                r1[i - 3] = product(nc.vector if i - 3 in R1_V else nc.gpsimd, two, "r1", f1[i - 3], w1t[i - 3])
-            if to_gain and i - 8 not in GAIN_V:
+            if r1_now:
+                multiply_r1(nc.gpsimd, i - 3)
+            if to_gain and not gain_on_vector(i - 8):
                 gain_tile(nc.gpsimd, *to_gain)
-            if new and i in W2_G:
-                nc.gpsimd.tensor_tensor(out=w2t[i][:, cut:], in0=s2[:, cut:], in1=s2[:, cut:], op=MULT)
+            if rung2_now and cut < width:
+                nc.gpsimd.tensor_tensor(out=w_rung2[i][:, cut:], in0=s2[:, cut:], in1=s2[:, cut:], op=MULT)
 
-            if mid:
-                u = i - 1
-                r2[u] = two.tile([P, WIDTHS[u // T]], F32, name="r2")
+            if f1_now:
+                unit = i - 1
+                r2[unit] = three.tile([P, WIDTHS[unit // T]], F32, name="r2")
                 nc.vector.scalar_tensor_tensor(
-                    out=r2[u][:], in0=a2[u][:], scalar=b_col(2, u), in1=w2t[u][:], op0=ADD, op1=MULT
+                    out=r2[unit][:],
+                    in0=a2[unit][:],
+                    scalar=bias_of(2, unit),
+                    in1=w_rung2[unit][:],
+                    op0=ADD,
+                    op1=MULT,
                 )
-            if to_scale and to_scale[0] > 0:
+            if to_scale:
                 scale_x_tile(*to_scale)
-            if out_:
+            if f0_now:
                 add_f0(i - 4)
-            if mid:
-                u = i - 1
-                f1[u] = four.tile([P, WIDTHS[u // T]], F32, name="f1")
+            if f1_now:
+                f1[unit] = five.tile([P, WIDTHS[unit // T]], F32, name="f1")
                 nc.vector.scalar_tensor_tensor(
-                    out=f1[u][:], in0=a1[u][:], scalar=b_col(1, u), in1=r2[u][:], op0=ADD, op1=ADD
+                    out=f1[unit][:],
+                    in0=a1[unit][:],
+                    scalar=bias_of(1, unit),
+                    in1=r2[unit][:],
+                    op0=ADD,
+                    op1=ADD,
                 )
-            if to_cast and to_cast[0] > 0:
-                cast_x(nc.vector.tensor_copy, *to_cast)
+            if to_widen:
+                widen_x(nc.vector.tensor_copy, *to_widen)
             if to_mix:
-                evict(nc.scalar.copy if i >= UNITS else nc.vector.tensor_copy, *to_mix)
-            if to_gain and i - 8 in GAIN_V:
+                store(nc.scalar.copy if i >= UNITS else nc.vector.tensor_copy, *to_mix)
+            if to_gain and gain_on_vector(i - 8):
                 gain_tile(nc.vector, *to_gain)
-            if to_code:
-                quantize_h(to_code[0], to_code[1], to_code[1] + 1)
-            if to_scale and to_scale[0] > 0:
-                quantize_x(to_scale[0], to_scale[1], to_scale[1] + 1)
+            if to_quantize:
+                quantize_h(*to_quantize)
+            if to_scale:
+                block, r = to_scale
+                quantize_x(block, r, r + 1)
+
             if i == -3:
-                copy_w2(1)
+                group(nc.vector.tensor_copy, weights2, raw_w2, 1)
             if i == -2:
-                copy_w2(2)
-                quantize_w(tw2, P, 2 * P)
+                group(nc.vector.tensor_copy, weights2, raw_w2, 2)
+                quantize_weights(weights2, P, 2 * P)
             if i == -1:
-                copy_w2(3)
-                quantize_w(tw2, 2 * P, 3 * P)
-                quantize_w(tw1, 0, L)
-                quantize_w(tw2, 3 * P, L)
-            if i == Q0_AT:
-                quantize_w(tw0, 0, L)
+                group(nc.vector.tensor_copy, weights2, raw_w2, 3)
+                quantize_weights(weights2, 2 * P, 3 * P)
+                quantize_weights(weights1, 0, L)
+                quantize_weights(weights2, 3 * P, L)
+            if i == 3:
+                quantize_weights(weights0, 0, L)
             if i == 4:
                 nc.vector.tensor_copy(
-                    out=tv[0][:].rearrange("p (c j) -> p c j", j=T), in_=raw_v[:].rearrange("p j c -> p c j")
+                    out=weights_v[0][:].rearrange("p (c j) -> p c j", j=T),
+                    in_=raw_v[:].rearrange("p j c -> p c j"),
                 )
             if i == 5:
-                quantize_w(tv, 0, O)
+                quantize_weights(weights_v, 0, O)
 
-        last, u = NB - 1, UNITS - 1
-        before = [t for t in (tile_at(s) for s in range(UNITS - 8, UNITS - 4)) if t]
-        final = [t for t in (tile_at(s) for s in range(UNITS - 4, UNITS)) if t]
-        gains = [t for t in (tile_at(s) for s in range(UNITS - 6, UNITS - 4)) if t]
-        codes = [t for t in (tile_at(s) for s in range(UNITS - 7, UNITS - 4)) if t]
-        f0_matmul(u - 1)
-        for t in before:
-            if t in gains:
-                gain_tile(nc.vector if UNITS - 8 + t[1] in GAIN_V else nc.gpsimd, *t)
-            if t in codes:
-                quantize_h(t[0], t[1], t[1] + 1)
-            mix(*t)
-            evict(nc.scalar.copy, *t)
-            if t == before[F0AT]:
-                add_f0(u - 1)
-                f0_matmul(u)
-        r1[u] = product(nc.vector, two, "r1", f1[u], w1t[u])
-        add_f0(u)
-        for t in final:
-            gain_tile(nc.vector if UNITS - 4 + 2 * t[1] in GAIN_V else nc.gpsimd, *t)
-        for t in final:
-            quantize_h(t[0], t[1], t[1] + 1)
-            mix(*t)
-            evict(nc.scalar.copy, *t)
+        last_unit = UNITS - 1
+        last, before = BLOCKS - 1, BLOCKS - 2
+        multiply_a0(last_unit - 1)
+        mix(before, 0)
+        store(nc.scalar.copy, before, 0)
+        gain_tile_by_scalar(before, 3)
+        quantize_h(before, 1)
+        gain_tile(nc.vector, before, 2)
+        add_f0(last_unit - 1)
+        multiply_a0(last_unit)
+        multiply_r1(nc.vector, last_unit)
+        quantize_h(before, 2)
+        mix_in_x_bank(before, 1)
+        store(nc.scalar.copy, before, 1)
+        mix_in_x_bank(before, 2)
+        add_f0(last_unit)
+        store(nc.scalar.copy, before, 2)
+        gain_tile(nc.vector, last, 0)
+        gain_tile(nc.vector, last, 1)
+        quantize_h(last, 0)
+        quantize_h(before, 3)
+        quantize_h(last, 1)
+        mix_in_x_bank(last, 0)
+        mix(before, 3)
+        mix_in_x_bank(last, 1)
+        store(nc.vector.tensor_copy, last, 0)
+        store(nc.scalar.copy, before, 3)
+        store(nc.vector.tensor_copy, last, 1)

from contextlib import ExitStack

import concourse.mybir as mybir
from concourse.masks import make_identity

N, D, L, O = 4096, 512, 512, 256
FLOPS = 2 * N * D * L * 3 + 2 * N * L * O

F32 = mybir.dt.float32
BF16 = mybir.dt.bfloat16
U32 = mybir.dt.uint32
U8 = mybir.dt.uint8
FP8 = mybir.dt.float8_e4m3fn
FP8X4 = mybir.dt.float8_e4m3fn_x4
ADD = mybir.AluOpType.add
MULT = mybir.AluOpType.mult
ACT = mybir.ActivationFunctionType

P = 128
T = 4

WIDTHS = (256, 512, 512, 512, 512, 512, 512, 512, 256)
BLOCKS = len(WIDTHS)
STARTS = tuple(sum(WIDTHS[:i]) for i in range(BLOCKS))
UNITS = BLOCKS * T

GPSIMD_COLUMNS = 96


def gain_on_vector(step):
    return step >= UNITS - 2 * T or step == UNITS - 3 * T


def token_tile_at(step):
    block, k = divmod(step, T)
    if not 0 <= block < BLOCKS:
        return None
    every = T * P // WIDTHS[block]
    return (block, k // every) if k % every == 0 else None


def tile_cofrnetladderlayer_t_kernel(tc, x_bytes, x_scale, w0, w1, w2, b, g, v, out):
    nc = tc.nc
    with ExitStack() as ctx:
        keep = ctx.enter_context(tc.tile_pool(name="keep", bufs=1))
        x_in = ctx.enter_context(tc.tile_pool(name="x_in", bufs=BLOCKS))
        three = ctx.enter_context(tc.tile_pool(name="three", bufs=3))
        four = ctx.enter_context(tc.tile_pool(name="four", bufs=4))
        five = ctx.enter_context(tc.tile_pool(name="five", bufs=5))
        p_a2 = ctx.enter_context(tc.psum_pool(name="p_a2", bufs=3))
        p_a1 = ctx.enter_context(tc.psum_pool(name="p_a1", bufs=1))
        p_a0 = ctx.enter_context(tc.psum_pool(name="p_a0", bufs=1))
        p_xt = ctx.enter_context(tc.psum_pool(name="p_xt", bufs=2))
        p_out = ctx.enter_context(tc.psum_pool(name="p_out", bufs=1))
        ctx.enter_context(tc.manual_schedule())

        x8 = {}

        def load_x(block):
            width = WIDTHS[block]
            x8[block] = x_in.tile([P, width // P, D], U8, name="x8")
            rows = x_bytes[STARTS[block] : STARTS[block] + width, :]
            nc.sync.dma_start(out=x8[block][:], in_=rows.rearrange("(p r) k -> p r k", p=P))

        def load_weights(w, name):
            raw = keep.tile([P, T, w.shape[1]], BF16, name="raw_" + name)
            nc.sync.dma_start(out=raw[:], in_=w.rearrange("(p j) c -> p j c", j=T))
            return raw

        load_x(0)
        raw_w1 = load_weights(w1, "w1")
        raw_w2 = load_weights(w2, "w2")
        load_x(1)
        raw_w0 = load_weights(w0, "w0")
        load_x(2)
        raw_v = load_weights(v, "v")
        for block in range(3, BLOCKS):
            load_x(block)

        scale_x = keep.tile([P, T], F32, name="scale_x")
        nc.scalar.dma_start(out=scale_x[:], in_=x_scale.rearrange("o (p t) -> p (o t)", t=T))
        raw_b = keep.tile([P, 3, T], BF16, name="raw_b")
        nc.scalar.dma_start(out=raw_b[:], in_=b.rearrange("i (p t) -> p i t", t=T))
        raw_g = keep.tile([P, T], BF16, name="raw_g")
        nc.scalar.dma_start(out=raw_g[:], in_=g.rearrange("(p t) -> p t", t=T))

        identity = keep.tile([P, P], F32, name="identity")
        make_identity(nc, identity[:])

        warm_in = keep.tile([P, 1], F32, name="warm_in")
        nc.vector.memset(warm_in[:], 1.0)
        warm_out = keep.tile([P, 1], F32, name="warm_out")
        nc.scalar.activation(out=warm_out[:], in_=warm_in[:], func=ACT.Abs_reciprocal_sqrt)

        bias = keep.tile([P, 3, T], F32, name="bias")
        gain = keep.tile([P, T], F32, name="gain")

        x_rows, x_turned, x_bf16, x_codes, x_scales = {}, {}, {}, {}, {}

        def widen_x(copy, block, r):
            if r == 0:
                x_rows[block] = three.tile([P, WIDTHS[block] // P, D], BF16, name="x_rows")
            copy(out=x_rows[block][:, r, :], in_=x8[block][:, r, :].bitcast(FP8))

        def turn_x(block, r):
            words = x_rows[block][:].bitcast(F32)
            x_turned[block, r] = p_xt.tile([P, 2, P], F32, name="xt")
            for u in range(2):
                nc.tensor.transpose(x_turned[block, r][:, u, :], words[:, r, u : D // 2 : 2], identity[:])

        def scale_x_tile(block, r):
            if r == 0:
                x_bf16[block] = three.tile([P, WIDTHS[block], T], BF16, name="x_bf16", align_bytes=64)
            nc.vector.tensor_tensor(
                out=x_bf16[block][:, r * P : (r + 1) * P, :].rearrange("p m (u e) -> p m u e", e=2),
                in0=x_turned[block, r][:].bitcast(BF16).rearrange("p u (m e) -> p m u e", e=2),
                in1=scale_x[:].unsqueeze(1).to_broadcast([P, P, T]).rearrange("p m (u e) -> p m u e", e=2),
                op=MULT,
            )

        def quantize_x(block, r0, r1):
            if r0 == 0:
                x_codes[block] = four.tile([P, WIDTHS[block]], U32, name="x_codes", align_bytes=64)
                x_scales[block] = four.tile([P, WIDTHS[block]], U8, name="x_scales", align_bytes=64)
            n = slice(r0 * P, r1 * P)
            nc.vector.quantize_mx(
                out=x_codes[block][:, n].bitcast(FP8X4),
                scales=x_scales[block][:, n],
                in_=x_bf16[block][:, n, :].rearrange("p m t -> p (m t)"),
            )

        def weight_tiles(name, width):
            return (
                keep.tile([P, T * width], BF16, name="bf16_" + name, align_bytes=64),
                keep.tile([P, width], U32, name="codes_" + name, align_bytes=64),
                keep.tile([P, width], U8, name="scales_" + name, align_bytes=64),
            )

        weights2 = weight_tiles("w2", L)
        weights1 = weight_tiles("w1", L)
        weights0 = weight_tiles("w0", L)
        weights_v = weight_tiles("v", O)

        def by_channel(raw):
            return raw[:].rearrange("p j (m t) -> p t m j", t=T)

        def grouped(tiles):
            return tiles[0][:].rearrange("p (t m j) -> p t m j", t=T, j=T)

        def group(copy, tiles, raw, t):
            copy(out=grouped(tiles)[:, t], in_=by_channel(raw)[:, t])

        def quantize_weights(tiles, c0, c1):
            bf16, codes, scales = tiles
            nc.vector.quantize_mx(
                out=codes[:, c0:c1].bitcast(FP8X4), scales=scales[:, c0:c1], in_=bf16[:, T * c0 : T * c1]
            )

        a2, a1, a0 = {}, {}, {}
        w_rung2, w_rung1 = {}, {}
        r2, f1, r1, f0 = {}, {}, {}, {}

        def multiply_x(pool, name, tiles, unit):
            block, t = divmod(unit, T)
            bank = pool.tile([P, WIDTHS[block]], F32, name=name)
            channels = slice(t * P, (t + 1) * P)
            nc.tensor.matmul_mx(
                out=bank[:],
                lhsT=tiles[1][:, channels].bitcast(FP8X4),
                lhsT_scale=tiles[2][:, channels],
                rhs=x_codes[block][:].bitcast(FP8X4),
                rhs_scale=x_scales[block][:],
                start=True,
                stop=True,
            )
            return bank

        def bias_of(rung, unit):
            t = unit % T
            return bias[:, rung, t : t + 1]

        def activate(name, src, func, bias_in):
            dst = four.tile([P, src.shape[1]], F32, name=name)
            nc.scalar.activation(out=dst[:], in_=src[:], func=func, bias=bias_in)
            return dst

        def multiply_r1(eng, unit):
            r1[unit] = three.tile([P, WIDTHS[unit // T]], F32, name="r1")
            eng.tensor_tensor(out=r1[unit][:], in0=f1[unit][:], in1=w_rung1[unit][:], op=MULT)

        def multiply_a0(unit):
            a0[unit] = multiply_x(p_a0, "a0", weights0, unit)

        def add_f0(unit):
            block, t = divmod(unit, T)
            if t == 0:
                f0[block] = three.tile([P, T, WIDTHS[block]], F32, name="f0")
            nc.vector.scalar_tensor_tensor(
                out=f0[block][:, t, :],
                in0=a0[unit][:],
                scalar=bias_of(0, unit),
                in1=r1[unit][:],
                op0=ADD,
                op1=ADD,
            )

        h_bf16, h_codes, h_scales, mixed, out_rows = {}, {}, {}, {}, {}

        def gain_tile(eng, block, r):
            if r == 0:
                h_bf16[block] = three.tile([P, WIDTHS[block], T], BF16, name="h_bf16", align_bytes=64)
            n = slice(r * P, (r + 1) * P)
            eng.tensor_tensor(
                out=h_bf16[block][:, n, :].rearrange("p (c i) t -> p c t i", i=4),
                in0=f0[block][:, :, n].rearrange("p t (c i) -> p c t i", i=4),
                in1=gain[:].unsqueeze(1).unsqueeze(3).to_broadcast([P, P // 4, T, 4]),
                op=MULT,
            )

        def gain_tile_by_scalar(block, r):
            n = slice(r * P, (r + 1) * P)
            for t in range(T):
                nc.scalar.activation(
                    out=h_bf16[block][:, n, t], in_=f0[block][:, t, n], func=ACT.Copy, scale=gain[:, t : t + 1]
                )

        def quantize_h(block, r):
            if r == 0:
                h_codes[block] = three.tile([P, WIDTHS[block]], U32, name="h_codes", align_bytes=64)
                h_scales[block] = three.tile([P, WIDTHS[block]], U8, name="h_scales", align_bytes=64)
            n = slice(r * P, (r + 1) * P)
            nc.vector.quantize_mx(
                out=h_codes[block][:, n].bitcast(FP8X4),
                scales=h_scales[block][:, n],
                in_=h_bf16[block][:, n, :].rearrange("p m t -> p (m t)"),
            )

        def mix_into(bank, block, r):
            mixed[block, r] = bank
            tokens = slice(r * P, (r + 1) * P)
            nc.tensor.matmul_mx(
                out=bank[:],
                lhsT=h_codes[block][:, tokens].bitcast(FP8X4),
                lhsT_scale=h_scales[block][:, tokens],
                rhs=weights_v[1][:].bitcast(FP8X4),
                rhs_scale=weights_v[2][:],
                start=True,
                stop=True,
            )

        def mix(block, r):
            bank = p_out.tile([P, O], F32, name="mixed")
            mix_into(bank, block, r)

        def mix_in_x_bank(block, r):
            bank = p_xt.tile([P, O], F32, name="xt")
            mix_into(bank, block, r)

        def store(copy, block, r):
            if r == 0:
                out_rows[block] = four.tile([P, WIDTHS[block] // P, O], F32, name="out_rows")
            copy(out=out_rows[block][:, r, :], in_=mixed[block, r][:])
            if r % 2 == 1:
                rows = out[STARTS[block] : STARTS[block] + WIDTHS[block], :].rearrange("(p r) o -> p r o", p=P)
                nc.sync.dma_start(out=rows[:, r - 1 : r + 1, :], in_=out_rows[block][:, r - 1 : r + 1, :])

        widen_x(nc.vector.tensor_copy, 0, 0)
        widen_x(nc.scalar.copy, 0, 1)
        turn_x(0, 0)
        turn_x(0, 1)
        nc.scalar.copy(out=grouped(weights1), in_=by_channel(raw_w1))
        scale_x_tile(0, 0)
        scale_x_tile(0, 1)
        nc.vector.tensor_copy(out=bias[:], in_=raw_b[:])
        nc.vector.tensor_copy(out=gain[:], in_=raw_g[:])
        group(nc.vector.tensor_copy, weights2, raw_w2, 0)
        quantize_x(0, 0, 2)
        quantize_weights(weights2, 0, P)
        a2[0] = multiply_x(p_a2, "a2", weights2, 0)

        for i in range(-3, UNITS + 2):
            rung2_now = 0 <= i < UNITS
            f1_now = 0 <= i - 1 < UNITS
            rung1_now = 0 <= i - 2 < UNITS
            r1_now = 0 <= i - 3 < UNITS
            f0_now = 0 <= i - 4 < UNITS
            to_widen, to_turn, to_scale = (t if t and t[0] > 0 else None for t in map(token_tile_at, (i + 7, i + 6, i + 5)))
            to_gain, to_quantize, to_mix = map(token_tile_at, (i - 8, i - 9, i - 10))

            if f0_now:
                multiply_a0(i - 4)
            if f1_now:
                a1[i - 1] = multiply_x(p_a1, "a1", weights1, i - 1)
            if to_turn:
                turn_x(*to_turn)
            if 0 <= i < UNITS - 1:
                a2[i + 1] = multiply_x(p_a2, "a2", weights2, i + 1)
            if to_mix:
                mix(*to_mix)

            if rung2_now:
                q2 = activate("q2", a2[i], ACT.Square, bias_of(2, i))
            if i in (0, 1):
                group(nc.scalar.copy, weights0, raw_w0, 2 * i)
            if rung1_now:
                q1 = activate("q1", f1[i - 2], ACT.Square, 0.0)
            if rung2_now:
                s2 = activate("s2", q2, ACT.Abs_reciprocal_sqrt, 0.5)
            if i in (0, 1):
                group(nc.scalar.copy, weights0, raw_w0, 2 * i + 1)
            if rung1_now:
                s1 = activate("s1", q1, ACT.Abs_reciprocal_sqrt, 0.5)
            if rung2_now:
                width = WIDTHS[i // T]
                cut = width - GPSIMD_COLUMNS if i < UNITS - T else width
                w_rung2[i] = four.tile([P, width], F32, name="w_rung2")
                nc.scalar.activation(out=w_rung2[i][:, :cut], in_=s2[:, :cut], func=ACT.Square)
            if rung1_now:
                w_rung1[i - 2] = activate("w_rung1", s1, ACT.Square, 0.0)

            if r1_now:
                multiply_r1(nc.gpsimd, i - 3)
            if to_gain and not gain_on_vector(i - 8):
                gain_tile(nc.gpsimd, *to_gain)
            if rung2_now and cut < width:
                nc.gpsimd.tensor_tensor(out=w_rung2[i][:, cut:], in0=s2[:, cut:], in1=s2[:, cut:], op=MULT)

            if f1_now:
                unit = i - 1
                r2[unit] = three.tile([P, WIDTHS[unit // T]], F32, name="r2")
                nc.vector.scalar_tensor_tensor(
                    out=r2[unit][:],
                    in0=a2[unit][:],
                    scalar=bias_of(2, unit),
                    in1=w_rung2[unit][:],
                    op0=ADD,
                    op1=MULT,
                )
            if to_scale:
                scale_x_tile(*to_scale)
            if f0_now:
                add_f0(i - 4)
            if f1_now:
                f1[unit] = five.tile([P, WIDTHS[unit // T]], F32, name="f1")
                nc.vector.scalar_tensor_tensor(
                    out=f1[unit][:],
                    in0=a1[unit][:],
                    scalar=bias_of(1, unit),
                    in1=r2[unit][:],
                    op0=ADD,
                    op1=ADD,
                )
            if to_widen:
                widen_x(nc.vector.tensor_copy, *to_widen)
            if to_mix:
                store(nc.scalar.copy if i >= UNITS else nc.vector.tensor_copy, *to_mix)
            if to_gain and gain_on_vector(i - 8):
                gain_tile(nc.vector, *to_gain)
            if to_quantize:
                quantize_h(*to_quantize)
            if to_scale:
                block, r = to_scale
                quantize_x(block, r, r + 1)

            if i == -3:
                group(nc.vector.tensor_copy, weights2, raw_w2, 1)
            if i == -2:
                group(nc.vector.tensor_copy, weights2, raw_w2, 2)
                quantize_weights(weights2, P, 2 * P)
            if i == -1:
                group(nc.vector.tensor_copy, weights2, raw_w2, 3)
                quantize_weights(weights2, 2 * P, 3 * P)
                quantize_weights(weights1, 0, L)
                quantize_weights(weights2, 3 * P, L)
            if i == 3:
                quantize_weights(weights0, 0, L)
            if i == 4:
                nc.vector.tensor_copy(
                    out=weights_v[0][:].rearrange("p (c j) -> p c j", j=T),
                    in_=raw_v[:].rearrange("p j c -> p c j"),
                )
            if i == 5:
                quantize_weights(weights_v, 0, O)

        last_unit = UNITS - 1
        last, before = BLOCKS - 1, BLOCKS - 2
        multiply_a0(last_unit - 1)
        mix(before, 0)
        store(nc.scalar.copy, before, 0)
        gain_tile_by_scalar(before, 3)
        quantize_h(before, 1)
        gain_tile(nc.vector, before, 2)
        add_f0(last_unit - 1)
        multiply_a0(last_unit)
        multiply_r1(nc.vector, last_unit)
        quantize_h(before, 2)
        mix_in_x_bank(before, 1)
        store(nc.scalar.copy, before, 1)
        mix_in_x_bank(before, 2)
        add_f0(last_unit)
        store(nc.scalar.copy, before, 2)
        gain_tile(nc.vector, last, 0)
        gain_tile(nc.vector, last, 1)
        quantize_h(last, 0)
        quantize_h(before, 3)
        quantize_h(last, 1)
        mix_in_x_bank(last, 0)
        mix(before, 3)
        mix_in_x_bank(last, 1)
        store(nc.vector.tensor_copy, last, 0)
        store(nc.scalar.copy, before, 3)
        store(nc.vector.tensor_copy, last, 1)
